import numpy as np, ml_dtypes
CORES = [16,17,18,19,32,33,34,35]
N = 8
import mx_ref
BF = ml_dtypes.bfloat16
def entries(a):
    return np.ascontiguousarray(a.T).reshape(-1)
def table(e):
    return np.ascontiguousarray(np.reshape(e, (-1, 16)).T).astype(np.int32)
def cols(t, e):
    v = np.concatenate([t.reshape(128, -1, 4), np.zeros((128, 1, 4), BF)], axis=1)
    return np.ascontiguousarray(v[:, e]).reshape(128, -1)
def f(rng, *shape):
    return mx_ref.flush((rng.standard_normal(shape, dtype=np.float32) * np.exp2(rng.integers(-2, 3, shape[:-1] + (1,)))).astype(BF))
def wide(rng, *shape, cols=0):
    v = rng.standard_normal(shape, dtype=np.float32) * np.exp2(rng.integers(-12, 13, shape)).astype(np.float32)
    if cols: v *= np.repeat(np.exp2(rng.integers(-cols, cols + 1, shape[:-2] + (1, shape[-1] // 4))) * (rng.random(shape[:-2] + (1, shape[-1] // 4)) > 0.0625), 4, axis=-1).astype(np.float32)
    return mx_ref.flush(v.astype(BF))
P, V, R, O, CAP, ALL = 256, 64, 4, 2, 14, 48
HOME = np.concatenate([np.repeat(np.arange(N), P), np.repeat(np.arange(N), V)])
def flat(a):
    return np.concatenate([entries(e) for e in a])
def game(alt, f1, f2):
    first, second = np.concatenate([np.arange(N * P), f1]), np.concatenate([alt, f2])
    stands = np.where(alt >= 0, np.arange(N * P), -1)
    k, leave, to, out = N * P + np.arange(N * V), np.repeat(np.arange(N), V), f1, []
    for t in range(R):
        was = stands[to]
        stands = np.array(stands); stands[to] = k
        out.append((k, leave, to, stands))
        k, at = was[was >= 0], to[was >= 0]
        leave, to = at // P, np.where(first[k] == at, second[k], first[k])
    return out
def draw(rng, lo, hi, aim):
    stands = np.full((N, P), -1)
    for r in range(N):
        p = rng.permutation(P)[:rng.integers(lo, hi + 1)]
        stands[r, p] = r * P + p
    if aim == "long":
        r = int(rng.integers(0, N)); stands[r] = r * P + np.arange(P)
    if aim == "short": stands[int(rng.integers(0, N))] = -1
    stands = stands.reshape(-1); start = stands >= 0
    first, second = np.concatenate([np.arange(N * P), np.full(N * V, -1)]), np.full(N * P + N * V, -1)
    came, total = np.zeros((N * P + N * V, N), bool), np.zeros((N, N), int)
    k, leave, at = N * P + np.arange(N * V), np.repeat(np.arange(N), V), np.full(N * V, -1)
    goal, last = int(rng.integers(0, N)), None
    mark, late = (goal + 1) % N, 0
    for t in range(R):
        used, free, to = np.zeros((N, N), int), np.ones(N * P, bool), np.full(len(k), -1)
        if aim == "long": mask = stands >= 0
        elif aim == "short" and t > 0: mask = stands < 0
        elif aim == "home" and t == 2: mask = np.isin(np.arange(N * P), last)
        elif aim == "peak": mask = np.arange(N * P) // P == goal
        else: mask = np.ones(N * P, bool)
        known = second[k] >= 0
        o = rng.permutation(len(k))
        if aim == "peak": o = np.concatenate([o[HOME[k[o]] == mark], o[HOME[k[o]] != mark]])
        for i in np.concatenate([o[known[o]], o[~known[o]]]):
            j, q, h = k[i], leave[i], HOME[k[i]]
            good = free & np.repeat((used[q] < CAP) & (came[j] | (total[h] < ALL) | (np.arange(N) == h)), P)
            if at[i] >= 0: good[at[i]] = False
            if known[i]:
                x = second[j] if first[j] == at[i] else first[j]
                if not good[x]: return None
            else:
                if (good & mask).any(): good = good & mask
                if not good.any(): return None
                x = rng.choice(np.flatnonzero(good))
                if t == 0: first[j] = x
                else: second[j] = x
            r = x // P
            to[i] = x; free[x] = False; used[q, r] += 1
            if r != h and not came[j, r]: total[h, r] += 1
            came[j, r] = True
        if aim == "long" and len(k) < N * V: return None
        if aim == "short" and ((t == 1 and len(k) == 0) or (t > 1 and len(k) > 0)): return None
        if aim == "home" and t == R - 1 and (to == k).sum() < N * V // 4: return None
        if aim == "peak" and t < 2 and (used[:, goal] < CAP).any(): return None
        if aim == "peak" and t >= 2: late = max(late, int(used[np.arange(N) != goal, goal].max()))
        was = stands[to]; stands[to] = k; last = to
        k, at = was[was >= 0], to[was >= 0]
        leave = at // P
    if aim == "peak" and (late < CAP - 4 or total[mark, goal] < ALL - 1): return None
    j = np.flatnonzero((second < 0) & np.concatenate([start, np.ones(N * V, bool)]))
    x = rng.integers(0, N * P - 1, len(j)); second[j] = x + (x >= first[j])
    return {"alt": np.stack([table(e) for e in second[:N * P].reshape(N, P)]), "f1": np.stack([table(e) for e in first[N * P:].reshape(N, V)]), "f2": np.stack([table(e) for e in second[N * P:].reshape(N, V)])}
def lists(rng, lo, hi, aim=None):
    for i in range(50):
        d = draw(rng, lo, hi, aim)
        if d is not None: return d
    raise RuntimeError("no draw in 50 tries")
def setup_inputs(rng):
    return {"c": f(rng, N, 128, 4 * P), "v": f(rng, N, 128, 4 * V), "w": f(rng, N, 128, 512 * R * O), **lists(rng, P // 2, 7 * P // 8)}
def setup_inputs_long(rng):
    return {**setup_inputs(rng), **lists(rng, 15 * P // 16, 31 * P // 32, "long")}
def setup_inputs_short(rng):
    return {**setup_inputs(rng), **lists(rng, P // 2, P // 2, "short")}
def setup_inputs_home(rng):
    return {**setup_inputs(rng), **lists(rng, 3 * P // 4, 3 * P // 4, "home")}
def setup_inputs_peak(rng):
    return {**setup_inputs(rng), **lists(rng, 7 * P // 8, 7 * P // 8, "peak")}
def setup_inputs_spread(rng):
    d = setup_inputs(rng); d["c"] = wide(rng, N, 128, 4 * P, cols=6); d["v"] = wide(rng, N, 128, 4 * V, cols=6); return d
def check_inputs(d):
    b = []
    alt, f1, f2 = flat(d["alt"]), flat(d["f1"]), flat(d["f2"])
    if alt.min() < -1 or alt.max() >= N * P or (alt == np.arange(N * P)).any(): b.append("alt")
    if f1.min() < 0 or f1.max() >= N * P: b.append("f1")
    if f2.min() < 0 or f2.max() >= N * P or (f1 == f2).any(): b.append("f2")
    if b: return b
    came = np.zeros((N * P + N * V, N), bool)
    for k, leave, to, stands in game(alt, f1, f2):
        if len(set(to.tolist())) != len(to): return b + ["two columns go to one place in one round"]
        n = np.zeros((N, N), int); np.add.at(n, (leave, to // P), 1)
        if n.max() > CAP: b.append("more than CAP columns from one rank to one rank in one round")
        came[k, to // P] = True
    for q in range(N):
        for r in range(N):
            if q != r and came[HOME == q, r].sum() > ALL: b.append("more than ALL columns of one rank come to another one")
    return b
def reference(c, v, w, alt, f1, f2):
    every = np.concatenate([c[r] for r in range(N)] + [v[r] for r in range(N)], axis=1)
    y = np.zeros((N, 128, R * O * P), np.float32)
    for t, (k, leave, to, stands) in enumerate(game(flat(alt), flat(f1), flat(f2))):
        for r in range(N):
            q = mx_ref.quantize(cols(every, stands[P * r:P * r + P]))
            for i in range(O * t, O * t + O):
                y[r][:, P * i:P * i + P] = mx_ref.matmul(mx_ref.quantize(w[r][:, 512 * i:512 * i + 512]), q)
    return {"y": y}

@@ -1,0 +1,447 @@
+from concourse.bass import DstId, RemoteDMATransfer
+from concourse.mybir import dt, AluOpType as A, ActivationFunctionType as F
+
+N, P, V, R, O = 8, 256, 64, 4, 2
+CH = N * V
+D0 = 512
+RS = P + 2 * V
+XW = D0 + N * P
+IDS = P + V
+ID0 = 8
+S0 = 512
+Z = 32
+E0, E1 = 16, 48
+OWN = Z + IDS
+W1 = OWN + (N - 1) * E0
+WW = W1 + (N - 1) * E1
+IT = P + V
+K0, K1 = 64, 200
+C0, C1 = 8, 22
+
+SCRATCH = {"lists": ("dram", [8, 128, 4], "float32"), "acc": ("psum", [128, 4096], "float32")}
+POOL = {}
+
+
+def _sb(dtype, **cols):
+    for k in cols:
+        SCRATCH[k] = ("sbuf", [128, cols[k]], dtype)
+        POOL[k] = (k, 0, cols[k])
+
+
+def _pool(buf, dtype, **cols):
+    a = 0
+    for k in cols:
+        POOL[k] = (buf, a, cols[k])
+        a += cols[k]
+    SCRATCH[buf] = ("sbuf", [128, a], dtype)
+
+
+_sb("int32", src=4, pi=1, row=RS, rowb=RS, hb=RS, jm=CH, jn=IT, dd=32)
+_sb("float32", sv=4, e16=4, md=RS, mask=CH, keep=CH, gm=CH, scn=CH, old1=CH, old2=CH, ones=CH, k32=IT, df=32, f1f=32, vf=4 * CH,
+    xt=XW, hz=XW, h4=XW, a0=P, x1s=P, ei=IT, mxi=IT, gg=IT, pf=IT, qq=IT, tq=IT, ts=IT, gn=V, gh=V, val=160, val0=32, pl0=208,
+    pl1=560, la0=C0, lb0=C0, la1=C1, lb1=C1, ch0=8, ch1=22, slot=S0 + ID0 + N * IDS + 24, sl0=(N - 1) * E0, sl1=(N - 1) * E1,
+    idw=64, gs=4 * P, gsc=4 * P, ys=2048)
+_sb("uint16", of1=32, ofq=32, ofz=32, ofw=32, ofp=10, ofp0=2, pk0u=C0, pk1u=C1, meta0=8, meta1=22, ofs0=8, ofs1=22, idu=64, so=64)
+_sb("bfloat16", cv=4 * OWN, wt=4096)
+_sb("float8_e4m3fn_x4", wq=1024, qo=OWN, sn0=128, sn1=352, fw=WW, pk0=P, pk1=P, pk2=P, pk3=P)
+_sb("uint8", wqs=1024, qos=OWN, sn0s=128, sn1s=352, fws=WW, ps0=P, ps1=P, ps2=P, ps3=P)
+_pool("tf", "float32", sxx=4, sxh=4, k2=4, k2a=4, sa=4, sb=4, sc=4, s1=4, s2=4, s3=4, sm=4, pif=1, c64=1, cm=1, c16=1, ck=1, pmf=1,
+      dc1=1, dcol=1, bg=1, h16=1, h48=1, b16=1, b48=1, ne2=V, ls0=C0, ls1=C1, m1=22, m2=22, m3=22, m4=22, m5=22, idy=64, idz=64)
+_pool("ti", "int32", sy=4, shh=4, pa3=1, pa2=1, pm=1, ri=10, lo=10, hi=10, l2=10, sm2=10, mx2=10, wi=32, wn=32, wm=32, idi=64, ids=64)
+SEMAPHORES = ["vv", "aa", "pp", "gq", "lsent", "aL", "aM0", "aC0", "aS0", "aM1", "aC1", "aS1", "dsrc", "drow", "dcv", "dw0", "dw1",
+              "down", "dfan", "df1", "dvf", "dpl0", "dpl1", "di0", "di1", "di2", "di3", "dy"]
+
+
+def rank_program(g, core, T, topo):
+    me = T.rank_of(core)
+    if me is None:
+        return
+    cores = T.cores
+    others = [d for d in range(N) if d != me]
+    OB = D0 + P * me
+    q = {"v": g.vector, "a": g.scalar, "p": g.tensor, "g": g, "y": g.sync}
+    csem = {"v": "vv", "a": "aa", "p": "pp", "g": "gq"}
+    cnt = {"v": 0, "a": 0, "p": 0, "g": 0}
+    known, wr, rd, pre = {}, {}, {}, {}
+
+    def b(name, r0=0, r1=128, c0=0, c1=None):
+        buf, a, w = POOL[name]
+        return T[buf][r0:r1, a + c0:a + (w if c1 is None else c1)]
+
+    def need(e, toks):
+        best = {}
+        for s, n in toks:
+            best[s] = max(best.get(s, 0), n)
+        for s in sorted(best):
+            if known.get((e, s), 0) < best[s]:
+                q[e].wait_ge(T.sem[s], best[s])
+                known[(e, s)] = best[s]
+
+    def op(e, fn, reads, writes, *args, **kw):
+        toks = []
+        for k in reads:
+            toks += wr.get(k, [])
+        for k in writes:
+            toks += wr.get(k, []) + rd.get(k, [])
+        need(e, toks)
+        cnt[e] += 1
+        fn(*args, **kw).then_inc(T.sem[csem[e]], 1)
+        tok = (csem[e], cnt[e])
+        for k in reads:
+            rd.setdefault(k, []).append(tok)
+        for k in writes:
+            wr[k], rd[k] = [tok], []
+
+    def dma(e, sem, total, reads, writes, out, in_):
+        tok, toks = (sem, total), []
+        for k in writes:
+            if wr.get(k) != [tok]:
+                pre[(sem, k)] = wr.get(k, []) + rd.get(k, [])
+                wr[k], rd[k] = [tok], []
+            toks += pre[(sem, k)]
+        for k in reads:
+            toks += wr.get(k, [])
+        need(e, toks)
+        q[e].dma_start(out, in_).then_inc(T.sem[sem], 16)
+        for k in reads:
+            rd.setdefault(k, []).append(tok)
+
+    def copy(reads, writes, out, in_, e="v"):
+        if e == "v":
+            op("v", g.vector.tensor_copy, reads, writes, out, in_)
+        else:
+            op("a", g.scalar.activation, reads, writes, out, in_, F.Copy)
+
+    def tsc(reads, writes, out, in0, s1, op0, s2=None, op1=None):
+        if op1 is None:
+            op("v", g.vector.tensor_scalar, reads, writes, out, in0, s1, None, op0)
+        else:
+            op("v", g.vector.tensor_scalar, reads, writes, out, in0, s1, s2, op0, op1)
+
+    def tt(reads, writes, out, in0, in1, o):
+        op("v", g.vector.tensor_tensor, reads, writes, out, in0, in1, o)
+
+    def tb(out, in0, in1, o):
+        tt([in0, in1], [out], b(out), b(in0), b(in1), o)
+
+    def sb(out, in0, s1, op0, s2=None, op1=None):
+        tsc([in0], [out], b(out), b(in0), s1, op0, s2, op1)
+
+    def scan(reads, writes, out, d0, d1, initial):
+        op("v", g.vector.tensor_tensor_scan, reads, writes, out, d0, d1, initial, A.mult, A.add)
+
+    def fill(key, ap, c):
+        op("v", g.vector.memset, [], [key], ap, c)
+
+    def iota(key, out, pattern, base, mult, f=True):
+        kw = {"allow_small_or_imprecise_dtypes": True} if f else {}
+        op("g", g.iota, [], [key], out, pattern, base, mult, **kw)
+
+    def engines(a, c):
+        off = [k for k in cores if k != a and topo.chip(k) != topo.chip(a)]
+        on = [k for k in cores if k != a and topo.chip(k) == topo.chip(a)]
+        far = topo.engines(a, off[0])
+        if c in off:
+            n, k = len(far) // len(off), off.index(c)
+            return far[n * k:n * k + n]
+        near = [x for x in topo.engines(a, c) if x not in far]
+        k = on.index(c)
+        return near[2 * k:2 * k + 2]
+
+    sent = [0]
+
+    def spread(sem, piece):
+        ts = []
+        for d in others:
+            src, dst = piece(d)
+            rid, pid = topo.addr(cores[d])[0:2]
+            m = 0
+            for x in engines(core, cores[d]):
+                m |= 1 << x
+                sent[0] += 1
+            ts.append(RemoteDMATransfer(dst_ids=[DstId(rid=rid, pnc=pid)], dma_engine_mask=m, remote_sem=T.sem[sem], src=src, dst=dst))
+        g.remote_dma_fused(ts, local_sem=T.sem.lsent)
+
+    def arrive(sem, key):
+        wr[key] = [(sem, sum(len(engines(cores[s], core)) for s in others))]
+
+    def at(s, d):
+        return s if s < d else s - 1
+
+    dma("y", "dsrc", 128, [], ["src"], T.src[0:64, :], T.alt[:, :])
+    dma("y", "dsrc", 128, [], ["src"], T.src[64:128, 0:1], T.f1[:, :])
+    dma("y", "dsrc", 128, [], ["src"], T.src[64:128, 1:2], T.f2[:, :])
+    for c in range(4):
+        dma("a", "dsrc", 128, [], ["src"], T.src[64 + c // 2:96:2, 2 + c % 2:3 + c % 2], T.f1[4 * c:4 * c + 4, :])
+    dma("y", "dsrc", 128, [], ["src"], T.src[96:128, 2:4], T.f1[:, :])
+    dma("a", "drow", 48, [], ["row"], T.row[0:1, 0:P], T.alt[:, :])
+    dma("a", "drow", 48, [], ["row"], T.row[0:1, P:IT], T.f2[:, :])
+    dma("a", "drow", 48, [], ["row"], T.row[0:1, IT:RS], T.f1[:, :])
+    dma("y", "dcv", 32, [], ["cv.c"], T.cv[:, 4 * Z:4 * (Z + P)], T.c[:, :])
+    dma("y", "dcv", 32, [], ["cv.c"], T.cv[:, 4 * (Z + P):4 * OWN], T.v[:, :])
+
+    iota("pi", b("pi"), [[1, 1]], 0, 1, False)
+    iota("e16", b("e16"), [[16, 4]], 0, 0)
+    iota("dd", b("dd"), [[16, 32]], 0, 1, False)
+    iota("f1o", b("f1f"), [[16, 32]], 0, 1)
+    iota("jm", b("jm"), [[0, 32], [1, 16]], 0, 0, False)
+
+    own0 = float(ID0 + IDS * me)
+    sb("pa3", "pi", 3, A.bitwise_and)
+    sb("pa2", "pi", 2, A.arith_shift_right)
+    fill("sxx", b("sxx"), 16.0)
+    fill("sxh", b("sxh"), 240.0)
+    fill("k2", b("k2", 64), float(D0))
+    sb("c64", "pa3", 64.0, A.mult)
+    sb("c16", "pa3", 16.0, A.mult)
+    fill("sxx", b("sxx", 64, 128, 0, 1), 16.0 + 4096.0)
+    fill("sxh", b("sxh", 64, 128, 0, 1), 240.0 + 4096.0 * (IDS - P))
+    fill("k2", b("k2", 64, 128, 0, 1), D0 + 4096.0 * ID0)
+    tb("cm", "c64", "pa2", A.add)
+    tb("ck", "c16", "pa2", A.add)
+    tsc(["e16", "cm"], ["k2a"], b("k2a", 0, 64), b("e16", 0, 64), b("cm", 0, 64), A.add, 4096.0, A.mult)
+    tsc(["ck"], ["k2"], b("k2", 64, 128, 1, 2), b("ck", 64), 4096.0, A.mult, D0 + 4096.0 * (own0 + P - 16), A.add)
+    tsc(["k2a"], ["k2"], b("k2", 0, 64), b("k2a", 0, 64), D0 + 4096.0 * own0, A.add)
+    copy(["pi"], ["pif"], b("pif"), b("pi"))
+
+    sb("sy", "src", 4, A.arith_shift_right)
+    sb("shh", "src", 8, A.arith_shift_right)
+    tb("sa", "src", "sxx", A.mult)
+    sb("sm", "src", 0.0, A.is_ge)
+    sb("sb", "sy", -255.0, A.mult)
+    tb("sc", "shh", "sxh", A.mult)
+    tb("s1", "sa", "k2", A.add)
+    tb("s2", "sb", "sc", A.add)
+    tb("s3", "s1", "s2", A.add)
+    tb("sv", "s3", "sm", A.mult)
+    need("g", wr["sv"])
+    spread("aL", lambda d: (b("sv"), T.lists[me]))
+    dma("y", "down", 16, ["sv"], ["lown"], T.lists[me], b("sv"))
+
+    op("g", g.partition_broadcast, ["row"], ["rowb"], T.rowb[0:32, :], T.row[0:1, :], 32)
+    iota("jn", b("jn"), [[0, 10], [1, 32]], 0, 0, False)
+    for r1, k in ((128, 4), (16, 0)):
+        iota("val0", b("val0", 0, r1), [[8, 2], [1, 4], [16, 4]], Z + P + k, 0)
+        iota("val.c", b("val", 0, r1, 0, 128), [[2, 8], [16, 16]], Z + k // 4, 0)
+        iota("val.v", b("val", 0, r1, 128, 160), [[8, 2], [1, 4], [16, 4]], Z + P + k, 0)
+    iota("df", b("df"), [[16, 32]], 0, 1)
+    for nm, w in (("ch0", 1), ("ch1", 3)):
+        if me > 0:
+            iota(nm, T[nm][:, 0:w * me], [[IDS, me], [0, w]], S0 + ID0 - Z, 0)
+        if me < N - 1:
+            iota(nm, T[nm][:, w * me:w * (N - 1)], [[IDS, N - 1 - me], [0, w]], S0 + ID0 - Z + IDS * (me + 1), 0)
+    iota("slot.own", b("slot", 0, 128, S0 + ID0 + IDS * me, S0 + ID0 + IDS * me + IDS), [[1, IDS]], Z, 0)
+    iota("sl0", b("sl0"), [[1, (N - 1) * E0]], OWN, 0)
+    iota("sl1", b("sl1"), [[1, (N - 1) * E1]], W1, 0)
+
+    fill("cv.z", T.cv[:, 0:4 * Z], 0.0)
+    fill("xt.d", T.xt[:, 0:640], 0.0)
+    fill("vf", b("vf"), 0.0)
+    fill("gg", T.gg[0:32, :], 0.0)
+    fill("ones", b("ones"), 1.0)
+    fill("pl0", b("pl0"), 0.0)
+    sb("dc1", "pif", float(me), A.is_equal, 99.0, A.mult)
+    tb("dcol", "dc1", "pif", A.add)
+    sb("bg", "pif", float(me), A.is_gt)
+    for nm, hh, e, k in (("b16", "h16", E0, K0), ("b48", "h48", E1, K1)):
+        tb(hh, "pif", "bg", A.subtract)
+        sb(nm, hh, float(e), A.mult, 16.0 * k - 1.0, A.add)
+    copy(["dd"], ["ofp0"], b("ofp0"), T.dd[:, 0:2])
+    copy(["dd"], ["ofp"], b("ofp"), T.dd[:, 0:10])
+    sb("k32", "jn", 0.0, A.is_gt)
+    tsc(["rowb"], ["hb"], T.hb[0:32, :], T.rowb[0:32, :], 8, A.arith_shift_right)
+    tsc(["hb", "dcol"], ["md"], T.md[0:32, :], T.hb[0:32, :], b("dcol", 0, 32), A.is_equal)
+
+    def compact(n, marks, key, base, width, of, val, vkeys, pl):
+        k = n // 32
+
+        def s(name, w=k):
+            return b(name, 0, 32, 0, w)
+        scan(["ones", base, key], ["pf"], s("pf", n), s("ones", n), marks, b(base, 0, 32))
+        tt(["pf", key], ["qq"], s("qq", n), s("pf", n), marks, A.mult)
+        op("v", g.vector.transpose, ["qq"], ["tq"], s("tq", n), s("qq", n))
+        scan(["tq", "k32"], ["ts"], s("ts", n), s("k32", n), s("tq", n), 0.0)
+        copy(["ts"], ["ri"], s("ri"), T.ts[0:32, 31:n:32])
+        tsc(["ri"], ["lo"], s("lo"), s("ri"), 15, A.bitwise_and)
+        tsc(["ri"], ["hi"], s("hi"), s("ri"), 4, A.arith_shift_right)
+        tsc(["lo"], ["l2"], s("l2"), s("lo"), float(width), A.mult)
+        tt(["l2", "hi"], ["sm2"], s("sm2"), s("l2"), s("hi"), A.add)
+        tt(["sm2", "dd"], ["mx2"], s("mx2"), s("sm2"), s("dd"), A.max)
+        copy(["mx2"], [of], s(of), s("mx2"))
+        copy([of] + vkeys, [pl], T[pl][:, :].indirect(T[of][:, 0:k]), T[val][:, :])
+
+    compact(V, T.md[0:32, IT:RS], "md", "b16", C0, "ofp0", "val0", ["val0"], "pl0")
+    for nm, r0 in (("la0", 0), ("lb0", 16)):
+        dma("g", "dpl0", 32, ["pl0"], [nm], b(nm), T.pl0[r0:r0 + 8, K0:K0 + 16 * C0])
+    tt(["hb"], ["ne2"], b("ne2", 0, 32), T.hb[0:32, P:IT], T.hb[0:32, IT:RS], A.not_equal)
+    tt(["ne2", "md"], ["md"], T.md[0:32, P:IT], T.md[0:32, P:IT], b("ne2", 0, 32), A.mult)
+    for dst, sc in (("qo", "qos"), ("fw", "fws")):
+        op("v", g.vector.quantize_mx, ["cv.z", "cv.c"], [dst + ".own"], T[dst][:, 0:OWN], T[sc][:, 0:OWN], T.cv[:, :])
+    sb("pm", "pi", 15, A.bitwise_and)
+    copy(["pm"], ["pmf"], b("pmf"), b("pm"))
+    tsc(["jm", "pmf"], ["mask"], b("mask"), b("jm"), b("pmf"), A.is_equal)
+    sb("keep", "jm", 0.0, A.is_gt)
+    fill("pl1", b("pl1"), 0.0)
+    fill("hz", b("hz"), 0.0)
+    fill("h4", T.h4[0:32, OB:OB + P], 0.0)
+    fill("slot.z", T.slot[:, S0:S0 + ID0], 0.0)
+
+    arrive("aL", "lfar")
+    for e, half in (("y", 0), ("a", 1)):
+        for p in range(8 * half, 8 * half + 8):
+            dma(e, "dfan", 256, ["lfar", "lown"], ["xt", "xt.d"], T.xt[p:p + 1, D0:XW], T.lists[:, 0:64, :])
+        for h in range(4 * half, 4 * half + 4):
+            dma(e, "df1", 128, ["lfar", "lown"], ["f1o"], T.f1f[0:16, 4 * h:4 * h + 4], T.lists[h, 64:96, 2:4])
+        for p in range(8 * half, 8 * half + 8):
+            dma(e, "dvf", 256, ["lfar", "lown"], ["vf"], T.vf[p:p + 1, :], T.lists[:, 64:128, :])
+    dma("y", "dw0", 16, [], ["wt0"], T.wt[:, 0:2048], T.w[:, 0:2048])
+    dma("a", "dw1", 16, [], ["wt1"], T.wt[:, 2048:4096], T.w[:, 2048:4096])
+
+    def look(table, keys, of, ok, gm, gk, n):
+        tt(keys + [ok, "mask"], [gk], gm, table.indirect(of), T.mask[:, 0:n], A.mult)
+
+    def diag(of):
+        scan(["gm", "keep"], ["scn"], b("scn"), b("keep"), b("gm"), 0.0)
+        copy(["scn"], ["wi"], b("wi"), T.scn[:, 15:CH:16])
+        sb("wn", "wi", 4095, A.bitwise_and)
+        tb("wm", "wn", "dd", A.max)
+        copy(["wm"], [of], b(of), b("wm"))
+
+    X = ["xt", "xt.d"]
+    tab = T.xt[:, :]
+    OX = T.xt[0:16, OB:OB + P]
+    v2, v1 = T.vf[:, 0:4 * CH:4], T.vf[:, 1:4 * CH:4]
+    copy(["xt"], ["a0"], T.a0[0:16, :], OX, "a")
+    copy(["f1o"], ["of1"], b("of1"), b("f1f"))
+    look(tab, X, b("of1"), "of1", b("gm"), "gm", CH)
+    diag("ofq")
+    copy(["vf", "of1"], X, tab.indirect(b("of1")), v1)
+    copy(["xt"], ["x1s"], T.x1s[0:16, :], OX, "a")
+    copy(X + ["ofq"], ["old1"], b("old1"), tab.indirect(b("ofq")), "a")
+    look(tab, X, b("ofq"), "ofq", b("gm"), "gm", CH)
+    diag("ofz")
+
+    def picks(k, first, e, w):
+        la, lb, ls, pku, dst, dss, meta = [x + k for x in ("la", "lb", "ls", "pk", "sn", "sn", "meta")]
+        pku, dss = pku + "u", dss + "s"
+        tb(ls, la, lb, A.add)
+        copy([ls], [pku], b(pku), b(ls))
+        copy(["qo.own", pku], [dst], b(dst).bitcast(dt.uint32), b("qo").bitcast(dt.uint32).indirect(b(pku)))
+        copy(["qo.own", pku], [dss], b(dss), b("qos").indirect(b(pku)), "a")
+        need("g", wr[pku])
+        spread("aM" + k, lambda d: (T[pku][:, w * at(d, me):w * at(d, me) + w], T[meta][:, w * at(me, d):w * at(me, d) + w]))
+        need("g", wr[dst])
+        spread("aC" + k, lambda d: (T[dst][:, e * at(d, me):e * at(d, me) + e].bitcast(dt.uint8),
+                                    T.fw[:, first + e * at(me, d):first + e * at(me, d) + e].bitcast(dt.uint8)))
+        need("g", wr[dss])
+        spread("aS" + k, lambda d: (T[dss][:, e * at(d, me):e * at(d, me) + e],
+                                    T.fws[:, first + e * at(me, d):first + e * at(me, d) + e]))
+        arrive("aM" + k, meta)
+        arrive("aC" + k, "fw" + k)
+        arrive("aS" + k, "fws" + k)
+
+    picks("0", OWN, E0, 1)
+
+    copy(["old1", "ofz"], ["hz"], b("hz").indirect(b("ofz")), b("old1"))
+    copy(["vf", "ofq"], X, tab.indirect(b("ofq")), v2)
+
+    own1 = T.of1[:, 4 * me:4 * me + 4]
+    copy(X + ["of1"], ["gn"], b("gn"), tab.indirect(own1))
+    copy(["hz", "of1"], ["gh"], b("gh"), b("hz").indirect(own1))
+    tt(["xt", "a0"], ["ei.c"], T.ei[0:16, 0:P], OX, T.a0[0:16, :], A.not_equal)
+    tt(["gn", "vf"], ["ei.v"], T.ei[0:16, P:IT], T.gn[0:16, :], T.vf[0:16, 4 * V * me + 1:4 * V * me + 4 * V:4], A.not_equal)
+    tt(["ei.c", "hz"], ["mxi.c"], T.mxi[0:16, 0:P], T.ei[0:16, 0:P], T.hz[0:16, OB:OB + P], A.max)
+    tt(["ei.v", "gh"], ["mxi.v"], T.mxi[0:16, P:IT], T.ei[0:16, P:IT], T.gh[0:16, :], A.max)
+    tt(["mxi.c", "mxi.v", "md"], ["gg"], T.gg[0:16, :], T.mxi[0:16, :], T.md[0:16, 0:IT], A.min)
+    compact(IT, T.gg[0:32, :], "gg", "b48", C1, "ofp", "val", ["val.c", "val.v"], "pl1")
+    for nm, r0, e in (("la1", 0, "y"), ("lb1", 16, "y")):
+        dma(e, "dpl1", 32, ["pl1"], [nm], b(nm), T.pl1[r0:r0 + 8, K1:K1 + 16 * C1])
+
+    fill("xt.d", T.xt[:, 0:D0], 0.0)
+    look(tab, X, b("ofz"), "ofz", b("gm"), "gm", CH)
+    copy(X + ["ofz"], ["old2"], b("old2"), tab.indirect(b("ofz")), "a")
+    diag("ofw")
+    dma("y", "di0", 16, ["x1s"], ["idw0"], T.idw[:, 0:16], T.x1s[0:8, :])
+    dma("y", "di1", 16, ["xt"], ["idw1"], T.idw[:, 16:32], T.xt[0:8, OB:OB + P])
+    dma("y", "di2", 16, ["hz"], ["idw2"], T.idw[:, 32:48], T.hz[0:8, OB:OB + P])
+
+    picks("1", W1, E1, 3)
+
+    def fill_slots(k, n):
+        meta, chn, of, vals = "meta" + k, "ch" + k, "ofs" + k, "sl" + k
+
+        def s(name):
+            return b(name, 0, 128, 0, n)
+        copy([meta], ["m1"], s("m1"), s(meta))
+        tsc(["m1"], ["m2"], s("m2"), s("m1"), 1.0, A.min)
+        tt(["m2", chn], ["m3"], s("m3"), s("m2"), s(chn), A.mult)
+        tt(["m3", "m1"], ["m4"], s("m4"), s("m3"), s("m1"), A.add)
+        tt(["m4", "df"], ["m5"], s("m5"), s("m4"), s("df"), A.max)
+        copy(["m5"], [of], s(of), s("m5"))
+        copy([of, vals], ["slot", "slot.own", "slot.z"], b("slot").indirect(s(of)), b(vals))
+
+    def slots(src, keys, c0, c1):
+        i, s = "idi%d" % c0, "ids%d" % c0
+        copy(keys, [i], b("idi", 0, 128, c0, c1), src)
+        tsc([i], [s], b("ids", 0, 128, c0, c1), b("idi", 0, 128, c0, c1), 12, A.arith_shift_right)
+        tsc([s], ["idu%d" % c0], T.idu[:, c0:c1], b("ids", 0, 128, c0, c1), float(S0), A.add)
+
+    def stand(t, key):
+        gk, w = "gs%d" % t, slice(P * t, P * t + P)
+        look(b("slot"), ["slot", "slot.own", "slot.z"], T.idu[:, 16 * t:16 * t + 16], key, T.gs[:, w], gk, P)
+        scan([gk, "keep"], [gk + "c"], T.gsc[:, w], T.keep[:, 0:P], T.gs[:, w], 0.0)
+        copy([gk + "c"], ["so%d" % t], T.so[:, 16 * t:16 * t + 16], T.gsc[:, P * t + 15:P * t + P:16])
+
+    def place(t):
+        n = W1 if t == 0 else WW
+        u = T.so[:, 16 * t:16 * t + 16]
+        pk, ps, ks = "pk%d" % t, "ps%d" % t, (["0"] if t == 0 else ["0", "1"])
+        copy(["fw.own", "so%d" % t] + ["fw" + k for k in ks], [pk], b(pk).bitcast(dt.uint32),
+             T.fw[:, 0:n].bitcast(dt.uint32).indirect(u))
+        copy(["fw.own", "so%d" % t] + ["fws" + k for k in ks], [ps], b(ps), T.fws[:, 0:n].indirect(u), "a")
+        for i in range(O * t, O * t + O):
+            w = slice(128 * i, 128 * i + 128)
+            op("p", g.tensor.matmul_mx, ["wq%d" % (i // 4), pk, ps], ["acc%d" % i], T.acc[:, 512 * i:512 * i + P],
+               T.wq[:, w], T.wqs[:, w], b(pk), b(ps), True, True)
+
+    def out(t):
+        for o in range(O):
+            i = O * t + o
+            w = slice(P * i, P * i + P)
+            copy(["acc%d" % i], ["ys%d" % i], T.ys[:, w], T.acc[:, 512 * i:512 * i + P], "va"[o])
+            dma("y", "dy", 16 * R * O, ["ys%d" % i], ["y%d" % i], T.y[:, w], T.ys[:, w])
+
+    copy(["old2", "ofw"], ["h4"], b("h4").indirect(b("ofw")), b("old2"))
+    dma("y", "di3", 16, ["h4"], ["idw3"], T.idw[:, 48:64], T.h4[0:8, OB:OB + P])
+    for h in range(2):
+        w = slice(512 * h, 512 * h + 512)
+        op("v", g.vector.quantize_mx, ["wt%d" % h], ["wq%d" % h], T.wq[:, w], T.wqs[:, w], T.wt[:, 2048 * h:2048 * h + 2048])
+    fill_slots("0", N - 1)
+    slots(T.idw[:, 0:16], ["idw0"], 0, 16)
+    stand(0, "idu0")
+    place(0)
+    out(0)
+    w1, w2, w3 = T.idw[:, 16:32], T.idw[:, 32:48], T.idw[:, 48:64]
+    y1, y2, y3 = [b("idy", 0, 128, 16 * k, 16 * k + 16) for k in (1, 2, 3)]
+    z0, z1, z2, z3 = [b("idz", 0, 128, 16 * k, 16 * k + 16) for k in range(4)]
+    copy(["idw1"], ["idy1"], y1, w1)
+    tsc(["idw2"], ["idz2"], z2, w2, 0.0, A.is_equal)
+    tt(["idz2", "idw1"], ["idz0"], z0, z2, w1, A.mult)
+    tt(["idz0", "idw2"], ["idy2"], y2, z0, w2, A.add)
+    slots(b("idy", 0, 128, 16, 48), ["idy1", "idy2"], 16, 48)
+    tsc(["idw3"], ["idz3"], z3, w3, 0.0, A.is_equal)
+    tt(["idz3", "idy2"], ["idz1"], z1, z3, y2, A.mult)
+    tt(["idz1", "idw3"], ["idy3"], y3, z1, w3, A.add)
+    slots(y3, ["idy3"], 48, 64)
+    fill_slots("1", 3 * (N - 1))
+    stand(1, "idu16")
+    stand(2, "idu16")
+    stand(3, "idu48")
+    place(1)
+    place(2)
+    out(1)
+    place(3)
+    out(2)
+    out(3)
+    need("y", [("dy", 16 * R * O)])
+    need("g", [("lsent", sent[0])])

@@ -3,7 +3,7 @@ from concourse.mybir import dt, AluOpType as A, ActivationFunctionType as F
 
 N, P, V, R, O = 8, 256, 64, 4, 2
 CH = N * V
-D0 = 512
+D0 = 2 * CH
 RS = P + 2 * V
 XW = D0 + N * P
 IDS = P + V
@@ -36,17 +36,18 @@ def _pool(buf, dtype, **cols):
     SCRATCH[buf] = ("sbuf", [128, a], dtype)
 
 
-_sb("int32", src=4, pi=1, row=RS, rowb=RS, hb=RS, jm=CH, jn=IT, dd=32)
-_sb("float32", sv=4, e16=4, md=RS, mask=CH, keep=CH, gm=CH, scn=CH, old1=CH, old2=CH, ones=CH, k32=IT, df=32, f1f=32, vf=4 * CH,
-    xt=XW, hz=XW, h4=XW, a0=P, x1s=P, ei=IT, mxi=IT, gg=IT, pf=IT, qq=IT, tq=IT, ts=IT, gn=V, gh=V, val=160, val0=32, pl0=208,
+_sb("int32", src=4, pi=1, row=RS, rowb=RS, hb=RS, jm=CH, jn=IT, dd=32, de=32, gli=20)
+_sb("float32", sv=4, e16=4, md=RS, mask=CH, keep=CH, gm=CH, scn=CH, old1=CH, old2=CH, ones=IT, k32=IT, df=32, f1f=32, vf=4 * CH,
+    xt=XW, a0=IT, x1s=P, x2s=P, x3s=P, ei=IT, gg=IT, pf=IT, qq=IT, tq=IT, ts=IT, val=160, val0=32, pl0=208,
     pl1=560, la0=C0, lb0=C0, la1=C1, lb1=C1, ch0=8, ch1=22, slot=S0 + ID0 + N * IDS + 24, sl0=(N - 1) * E0, sl1=(N - 1) * E1,
     idw=64, gs=4 * P, gsc=4 * P, ys=2048)
-_sb("uint16", of1=32, ofq=32, ofz=32, ofw=32, ofp=10, ofp0=2, pk0u=C0, pk1u=C1, meta0=8, meta1=22, ofs0=8, ofs1=22, idu=64, so=64)
+_sb("uint16", of1=32, ofq=32, ofz=32, ofw=32, gl=20, ofp=10, ofp0=2, pk0u=C0, pk1u=C1, meta0=8, meta1=22, ofs0=8, ofs1=22, idu=64,
+    so=64)
 _sb("bfloat16", cv=4 * OWN, wt=4096)
 _sb("float8_e4m3fn_x4", wq=1024, qo=OWN, sn0=128, sn1=352, fw=WW, pk0=P, pk1=P, pk2=P, pk3=P)
 _sb("uint8", wqs=1024, qos=OWN, sn0s=128, sn1s=352, fws=WW, ps0=P, ps1=P, ps2=P, ps3=P)
 _pool("tf", "float32", sxx=4, sxh=4, k2=4, k2a=4, sa=4, sb=4, sc=4, s1=4, s2=4, s3=4, sm=4, pif=1, c64=1, cm=1, c16=1, ck=1, pmf=1,
-      dc1=1, dcol=1, bg=1, h16=1, h48=1, b16=1, b48=1, ne2=V, ls0=C0, ls1=C1, m1=22, m2=22, m3=22, m4=22, m5=22, idy=64, idz=64)
+      dc1=1, dcol=1, bg=1, h16=1, h48=1, b16=1, b48=1, ne2=V, ls0=C0, ls1=C1, m1=22, m2=22, m3=22, m4=22, m5=22)
 _pool("ti", "int32", sy=4, shh=4, pa3=1, pa2=1, pm=1, ri=10, lo=10, hi=10, l2=10, sm2=10, mx2=10, wi=32, wn=32, wm=32, idi=64, ids=64)
 SEMAPHORES = ["vv", "aa", "pp", "gq", "lsent", "aL", "aM0", "aC0", "aS0", "aM1", "aC1", "aS1", "dsrc", "drow", "dcv", "dw0", "dw1",
               "down", "dfan", "df1", "dvf", "dpl0", "dpl1", "di0", "di1", "di2", "di3", "dy"]
@@ -186,6 +187,7 @@ def rank_program(g, core, T, topo):
     iota("f1o", b("f1f"), [[16, 32]], 0, 1)
     iota("jm", b("jm"), [[0, 32], [1, 16]], 0, 0, False)
 
+    fill("xt.d", T.xt[:, 0:D0 + 128], 0.0)
     own0 = float(ID0 + IDS * me)
     sb("pa3", "pi", 3, A.bitwise_and)
     sb("pa2", "pi", 2, A.arith_shift_right)
@@ -202,7 +204,10 @@ def rank_program(g, core, T, topo):
     tsc(["e16", "cm"], ["k2a"], b("k2a", 0, 64), b("e16", 0, 64), b("cm", 0, 64), A.add, 4096.0, A.mult)
     tsc(["ck"], ["k2"], b("k2", 64, 128, 1, 2), b("ck", 64), 4096.0, A.mult, D0 + 4096.0 * (own0 + P - 16), A.add)
     tsc(["k2a"], ["k2"], b("k2", 0, 64), b("k2a", 0, 64), D0 + 4096.0 * own0, A.add)
-    copy(["pi"], ["pif"], b("pif"), b("pi"))
+    for k in range(2):
+        copy(["xt.d"], ["vf"], T.vf[:, D0 * k:D0 * k + D0], T.xt[:, 0:D0], "a")
+    copy(["xt.d"], ["a0"], b("a0"), T.xt[:, 0:IT], "a")
+    copy(["xt.d"], ["pl1"], b("pl1"), T.xt[:, 0:560], "a")
 
     sb("sy", "src", 4, A.arith_shift_right)
     sb("shh", "src", 8, A.arith_shift_right)
@@ -222,6 +227,10 @@ def rank_program(g, core, T, topo):
     iota("jn", b("jn"), [[0, 10], [1, 32]], 0, 0, False)
     for r1, k in ((128, 4), (16, 0)):
         iota("val0", b("val0", 0, r1), [[8, 2], [1, 4], [16, 4]], Z + P + k, 0)
+    iota("de", b("de"), [[16, 32]], CH, 1, False)
+    iota("gli", b("gli"), [[16, 20]], 0, 1, False)
+    iota("gli", b("gli", 0, 16), [[16, 20]], OB, 1, False)
+    for r1, k in ((128, 4), (16, 0)):
         iota("val.c", b("val", 0, r1, 0, 128), [[2, 8], [16, 16]], Z + k // 4, 0)
         iota("val.v", b("val", 0, r1, 128, 160), [[8, 2], [1, 4], [16, 4]], Z + P + k, 0)
     iota("df", b("df"), [[16, 32]], 0, 1)
@@ -235,11 +244,10 @@ def rank_program(g, core, T, topo):
     iota("sl1", b("sl1"), [[1, (N - 1) * E1]], W1, 0)
 
     fill("cv.z", T.cv[:, 0:4 * Z], 0.0)
-    fill("xt.d", T.xt[:, 0:640], 0.0)
-    fill("vf", b("vf"), 0.0)
-    fill("gg", T.gg[0:32, :], 0.0)
     fill("ones", b("ones"), 1.0)
     fill("pl0", b("pl0"), 0.0)
+    fill("slot.z", T.slot[:, S0:S0 + ID0], 0.0)
+    copy(["pi"], ["pif"], b("pif"), b("pi"))
     sb("dc1", "pif", float(me), A.is_equal, 99.0, A.mult)
     tb("dcol", "dc1", "pif", A.add)
     sb("bg", "pif", float(me), A.is_gt)
@@ -248,6 +256,12 @@ def rank_program(g, core, T, topo):
         sb(nm, hh, float(e), A.mult, 16.0 * k - 1.0, A.add)
     copy(["dd"], ["ofp0"], b("ofp0"), T.dd[:, 0:2])
     copy(["dd"], ["ofp"], b("ofp"), T.dd[:, 0:10])
+    sb("pm", "pi", 15, A.bitwise_and)
+    copy(["pm"], ["pmf"], b("pmf"), b("pm"))
+    tsc(["jm", "pmf"], ["mask"], b("mask"), b("jm"), b("pmf"), A.is_equal)
+    sb("keep", "jm", 0.0, A.is_gt)
+    for dst, sc in (("qo", "qos"), ("fw", "fws")):
+        op("v", g.vector.quantize_mx, ["cv.z", "cv.c"], [dst + ".own"], T[dst][:, 0:OWN], T[sc][:, 0:OWN], T.cv[:, :])
     sb("k32", "jn", 0.0, A.is_gt)
     tsc(["rowb"], ["hb"], T.hb[0:32, :], T.rowb[0:32, :], 8, A.arith_shift_right)
     tsc(["hb", "dcol"], ["md"], T.md[0:32, :], T.hb[0:32, :], b("dcol", 0, 32), A.is_equal)
@@ -275,16 +289,7 @@ def rank_program(g, core, T, topo):
         dma("g", "dpl0", 32, ["pl0"], [nm], b(nm), T.pl0[r0:r0 + 8, K0:K0 + 16 * C0])
     tt(["hb"], ["ne2"], b("ne2", 0, 32), T.hb[0:32, P:IT], T.hb[0:32, IT:RS], A.not_equal)
     tt(["ne2", "md"], ["md"], T.md[0:32, P:IT], T.md[0:32, P:IT], b("ne2", 0, 32), A.mult)
-    for dst, sc in (("qo", "qos"), ("fw", "fws")):
-        op("v", g.vector.quantize_mx, ["cv.z", "cv.c"], [dst + ".own"], T[dst][:, 0:OWN], T[sc][:, 0:OWN], T.cv[:, :])
-    sb("pm", "pi", 15, A.bitwise_and)
-    copy(["pm"], ["pmf"], b("pmf"), b("pm"))
-    tsc(["jm", "pmf"], ["mask"], b("mask"), b("jm"), b("pmf"), A.is_equal)
-    sb("keep", "jm", 0.0, A.is_gt)
-    fill("pl1", b("pl1"), 0.0)
-    fill("hz", b("hz"), 0.0)
-    fill("h4", T.h4[0:32, OB:OB + P], 0.0)
-    fill("slot.z", T.slot[:, S0:S0 + ID0], 0.0)
+    copy(["gli"], ["gl"], T.gl[:, 0:16], T.gli[:, 0:16])
 
     arrive("aL", "lfar")
     for e, half in (("y", 0), ("a", 1)):
@@ -300,26 +305,30 @@ def rank_program(g, core, T, topo):
     def look(table, keys, of, ok, gm, gk, n):
         tt(keys + [ok, "mask"], [gk], gm, table.indirect(of), T.mask[:, 0:n], A.mult)
 
-    def diag(of):
+    def diag(of, dump):
         scan(["gm", "keep"], ["scn"], b("scn"), b("keep"), b("gm"), 0.0)
         copy(["scn"], ["wi"], b("wi"), T.scn[:, 15:CH:16])
         sb("wn", "wi", 4095, A.bitwise_and)
-        tb("wm", "wn", "dd", A.max)
+        tb("wm", "wn", dump, A.max)
         copy(["wm"], [of], b(of), b("wm"))
 
     X = ["xt", "xt.d"]
     tab = T.xt[:, :]
     OX = T.xt[0:16, OB:OB + P]
     v2, v1 = T.vf[:, 0:4 * CH:4], T.vf[:, 1:4 * CH:4]
-    copy(["xt"], ["a0"], T.a0[0:16, :], OX, "a")
+    copy(["xt"], ["a0"], T.a0[0:16, 0:P], OX, "a")
+    copy(["vf"], ["a0v"], T.a0[0:16, P:IT], T.vf[0:16, 4 * V * me + 1:4 * V * me + 4 * V:4], "a")
     copy(["f1o"], ["of1"], b("of1"), b("f1f"))
     look(tab, X, b("of1"), "of1", b("gm"), "gm", CH)
-    diag("ofq")
+    diag("ofq", "dd")
     copy(["vf", "of1"], X, tab.indirect(b("of1")), v1)
     copy(["xt"], ["x1s"], T.x1s[0:16, :], OX, "a")
     copy(X + ["ofq"], ["old1"], b("old1"), tab.indirect(b("ofq")), "a")
     look(tab, X, b("ofq"), "ofq", b("gm"), "gm", CH)
-    diag("ofz")
+    diag("ofz", "de")
+    copy(["vf", "ofq"], X, tab.indirect(b("ofq")), v2)
+    copy(X + ["ofz"], ["old2"], b("old2"), tab.indirect(b("ofz")), "a")
+    copy(["xt"], ["x2s"], T.x2s[0:16, :], OX, "a")
 
     def picks(k, first, e, w):
         la, lb, ls, pku, dst, dss, meta = [x + k for x in ("la", "lb", "ls", "pk", "sn", "sn", "meta")]
@@ -341,29 +350,24 @@ def rank_program(g, core, T, topo):
         arrive("aS" + k, "fws" + k)
 
     picks("0", OWN, E0, 1)
+    copy(["of1"], ["gl.v"], T.gl[:, 16:20], T.of1[:, 4 * me:4 * me + 4])
+    for h in range(2):
+        w = slice(512 * h, 512 * h + 512)
+        op("v", g.vector.quantize_mx, ["wt%d" % h], ["wq%d" % h], T.wq[:, w], T.wqs[:, w], T.wt[:, 2048 * h:2048 * h + 2048])
+    copy(["old1", "ofz"], X, tab.indirect(b("ofz")), b("old1"))
 
-    copy(["old1", "ofz"], ["hz"], b("hz").indirect(b("ofz")), b("old1"))
-    copy(["vf", "ofq"], X, tab.indirect(b("ofq")), v2)
-
-    own1 = T.of1[:, 4 * me:4 * me + 4]
-    copy(X + ["of1"], ["gn"], b("gn"), tab.indirect(own1))
-    copy(["hz", "of1"], ["gh"], b("gh"), b("hz").indirect(own1))
-    tt(["xt", "a0"], ["ei.c"], T.ei[0:16, 0:P], OX, T.a0[0:16, :], A.not_equal)
-    tt(["gn", "vf"], ["ei.v"], T.ei[0:16, P:IT], T.gn[0:16, :], T.vf[0:16, 4 * V * me + 1:4 * V * me + 4 * V:4], A.not_equal)
-    tt(["ei.c", "hz"], ["mxi.c"], T.mxi[0:16, 0:P], T.ei[0:16, 0:P], T.hz[0:16, OB:OB + P], A.max)
-    tt(["ei.v", "gh"], ["mxi.v"], T.mxi[0:16, P:IT], T.ei[0:16, P:IT], T.gh[0:16, :], A.max)
-    tt(["mxi.c", "mxi.v", "md"], ["gg"], T.gg[0:16, :], T.mxi[0:16, :], T.md[0:16, 0:IT], A.min)
+    tt(X + ["gl", "gl.v", "a0", "a0v"], ["ei"], b("ei"), tab.indirect(b("gl")), b("a0"), A.not_equal)
+    tt(["ei", "md"], ["gg"], T.gg[0:32, :], T.ei[0:32, :], T.md[0:32, 0:IT], A.mult)
     compact(IT, T.gg[0:32, :], "gg", "b48", C1, "ofp", "val", ["val.c", "val.v"], "pl1")
-    for nm, r0, e in (("la1", 0, "y"), ("lb1", 16, "y")):
-        dma(e, "dpl1", 32, ["pl1"], [nm], b(nm), T.pl1[r0:r0 + 8, K1:K1 + 16 * C1])
+    for nm, r0 in (("la1", 0), ("lb1", 16)):
+        dma("y", "dpl1", 32, ["pl1"], [nm], b(nm), T.pl1[r0:r0 + 8, K1:K1 + 16 * C1])
 
-    fill("xt.d", T.xt[:, 0:D0], 0.0)
-    look(tab, X, b("ofz"), "ofz", b("gm"), "gm", CH)
-    copy(X + ["ofz"], ["old2"], b("old2"), tab.indirect(b("ofz")), "a")
-    diag("ofw")
-    dma("y", "di0", 16, ["x1s"], ["idw0"], T.idw[:, 0:16], T.x1s[0:8, :])
-    dma("y", "di1", 16, ["xt"], ["idw1"], T.idw[:, 16:32], T.xt[0:8, OB:OB + P])
-    dma("y", "di2", 16, ["hz"], ["idw2"], T.idw[:, 32:48], T.hz[0:8, OB:OB + P])
+    copy(["xt"], ["x3s"], T.x3s[0:16, :], OX, "a")
+    tb("gm", "old2", "mask", A.mult)
+    diag("ofw", "dd")
+    for t in range(3):
+        nm = "x%ds" % (t + 1)
+        dma("y", "di%d" % t, 16, [nm], ["idw%d" % t], T.idw[:, 16 * t:16 * t + 16], T[nm][0:8, :])
 
     picks("1", W1, E1, 3)
 
@@ -380,9 +384,9 @@ def rank_program(g, core, T, topo):
         copy(["m5"], [of], s(of), s("m5"))
         copy([of, vals], ["slot", "slot.own", "slot.z"], b("slot").indirect(s(of)), b(vals))
 
-    def slots(src, keys, c0, c1):
+    def slots(keys, c0, c1):
         i, s = "idi%d" % c0, "ids%d" % c0
-        copy(keys, [i], b("idi", 0, 128, c0, c1), src)
+        copy(keys, [i], b("idi", 0, 128, c0, c1), T.idw[:, c0:c1])
         tsc([i], [s], b("ids", 0, 128, c0, c1), b("idi", 0, 128, c0, c1), 12, A.arith_shift_right)
         tsc([s], ["idu%d" % c0], T.idu[:, c0:c1], b("ids", 0, 128, c0, c1), float(S0), A.add)
 
@@ -411,33 +415,20 @@ def rank_program(g, core, T, topo):
             copy(["acc%d" % i], ["ys%d" % i], T.ys[:, w], T.acc[:, 512 * i:512 * i + P], "va"[o])
             dma("y", "dy", 16 * R * O, ["ys%d" % i], ["y%d" % i], T.y[:, w], T.ys[:, w])
 
-    copy(["old2", "ofw"], ["h4"], b("h4").indirect(b("ofw")), b("old2"))
-    dma("y", "di3", 16, ["h4"], ["idw3"], T.idw[:, 48:64], T.h4[0:8, OB:OB + P])
-    for h in range(2):
-        w = slice(512 * h, 512 * h + 512)
-        op("v", g.vector.quantize_mx, ["wt%d" % h], ["wq%d" % h], T.wq[:, w], T.wqs[:, w], T.wt[:, 2048 * h:2048 * h + 2048])
+    copy(["old2", "ofw"], X, tab.indirect(b("ofw")), b("old2"))
+    dma("y", "di3", 16, ["xt"], ["idw3"], T.idw[:, 48:64], T.xt[0:8, OB:OB + P])
     fill_slots("0", N - 1)
-    slots(T.idw[:, 0:16], ["idw0"], 0, 16)
+    slots(["idw0"], 0, 16)
     stand(0, "idu0")
     place(0)
     out(0)
-    w1, w2, w3 = T.idw[:, 16:32], T.idw[:, 32:48], T.idw[:, 48:64]
-    y1, y2, y3 = [b("idy", 0, 128, 16 * k, 16 * k + 16) for k in (1, 2, 3)]
-    z0, z1, z2, z3 = [b("idz", 0, 128, 16 * k, 16 * k + 16) for k in range(4)]
-    copy(["idw1"], ["idy1"], y1, w1)
-    tsc(["idw2"], ["idz2"], z2, w2, 0.0, A.is_equal)
-    tt(["idz2", "idw1"], ["idz0"], z0, z2, w1, A.mult)
-    tt(["idz0", "idw2"], ["idy2"], y2, z0, w2, A.add)
-    slots(b("idy", 0, 128, 16, 48), ["idy1", "idy2"], 16, 48)
-    tsc(["idw3"], ["idz3"], z3, w3, 0.0, A.is_equal)
-    tt(["idz3", "idy2"], ["idz1"], z1, z3, y2, A.mult)
-    tt(["idz1", "idw3"], ["idy3"], y3, z1, w3, A.add)
-    slots(y3, ["idy3"], 48, 64)
+    slots(["idw1", "idw2"], 16, 48)
     fill_slots("1", 3 * (N - 1))
     stand(1, "idu16")
     stand(2, "idu16")
-    stand(3, "idu48")
     place(1)
+    slots(["idw3"], 48, 64)
+    stand(3, "idu48")
     place(2)
     out(1)
     place(3)

@@ -17,6 +17,7 @@ WW = W1 + (N - 1) * E1
 IT = P + V
 K0, K1 = 64, 200
 C0, C1 = 8, 22
+W = {"0": 1, "1": 3}
 
 SCRATCH = {"lists": ("dram", [8, 128, 4], "float32"), "acc": ("psum", [128, 4096], "float32")}
 POOL = {}
@@ -37,18 +38,18 @@ def _pool(buf, dtype, **cols):
 
 
 _sb("int32", src=4, pi=1, row=RS, rowb=RS, hb=RS, jm=CH, jn=IT, dd=32, de=32, gli=20)
-_sb("float32", sv=4, e16=4, md=RS, mask=CH, keep=CH, gm=CH, scn=CH, old1=CH, old2=CH, ones=IT, k32=IT, df=32, f1f=32, vf=4 * CH,
-    xt=XW, a0=IT, x1s=P, x2s=P, x3s=P, ei=IT, gg=IT, pf=IT, qq=IT, tq=IT, ts=IT, val=160, val0=32, pl0=208,
-    pl1=560, la0=C0, lb0=C0, la1=C1, lb1=C1, ch0=8, ch1=22, slot=S0 + ID0 + N * IDS + 24, sl0=(N - 1) * E0, sl1=(N - 1) * E1,
+_sb("float32", sv=4, e16=4, md=RS, mask=CH, keep=CH, gm=CH, scn=CH, old1=CH, old2=CH, ones=IT, k32=IT, df0=8, df1=22, f1f=32,
+    vf=4 * CH, xt=XW, a0=IT, x1s=P, x2s=P, x3s=P, ei=IT, gg=IT, pf=IT, qq=IT, tq=IT, ts=IT, val=160, val0=32, pl0=208,
+    pl1=560, la0=C0, lb0=C0, la1=C1, lb1=C1, slot=S0 + ID0 + N * IDS + 24, sl0=(N - 1) * E0, sl1=(N - 1) * E1,
     idw=64, gs=4 * P, gsc=4 * P, ys=2048)
-_sb("uint16", of1=32, ofq=32, ofz=32, ofw=32, gl=20, ofp=10, ofp0=2, pk0u=C0, pk1u=C1, meta0=8, meta1=22, ofs0=8, ofs1=22, idu=64,
+_sb("uint16", of1=32, ofq=32, ofz=32, ofw=32, gl=20, ofp=10, ofp0=2, pk0u=C0, pk1u=C1, mt0u=8, mt1u=22, meta0=8, meta1=22, idu=64,
     so=64)
 _sb("bfloat16", cv=4 * OWN, wt=4096)
 _sb("float8_e4m3fn_x4", wq=1024, qo=OWN, sn0=128, sn1=352, fw=WW, pk0=P, pk1=P, pk2=P, pk3=P)
 _sb("uint8", wqs=1024, qos=OWN, sn0s=128, sn1s=352, fws=WW, ps0=P, ps1=P, ps2=P, ps3=P)
 _pool("tf", "float32", sxx=4, sxh=4, k2=4, k2a=4, sa=4, sb=4, sc=4, s1=4, s2=4, s3=4, sm=4, pif=1, c64=1, cm=1, c16=1, ck=1, pmf=1,
-      dc1=1, dcol=1, bg=1, h16=1, h48=1, b16=1, b48=1, ne2=V, ls0=C0, ls1=C1, m1=22, m2=22, m3=22, m4=22, m5=22)
-_pool("ti", "int32", sy=4, shh=4, pa3=1, pa2=1, pm=1, ri=10, lo=10, hi=10, l2=10, sm2=10, mx2=10, wi=32, wn=32, wm=32, idi=64, ids=64)
+      dc1=1, dcol=1, bg=1, h16=1, h48=1, b16=1, b48=1, ne2=V, ls0=C0, ls1=C1, mt0=8, mt1=22)
+_pool("ti", "int32", sy=4, shh=4, pa3=1, pa2=1, pm=1, lo=10, hi=10, l2=10, sm2=10, mx2=10, wi=32, wn=32, wm=32, ids=64)
 SEMAPHORES = ["vv", "aa", "pp", "gq", "lsent", "aL", "aM0", "aC0", "aS0", "aM1", "aC1", "aS1", "dsrc", "drow", "dcv", "dw0", "dw1",
               "down", "dfan", "df1", "dvf", "dpl0", "dpl1", "di0", "di1", "di2", "di3", "dy"]
 
@@ -60,6 +61,7 @@ def rank_program(g, core, T, topo):
     cores = T.cores
     others = [d for d in range(N) if d != me]
     OB = D0 + P * me
+    SM = S0 + ID0 + IDS * me - Z
     q = {"v": g.vector, "a": g.scalar, "p": g.tensor, "g": g, "y": g.sync}
     csem = {"v": "vv", "a": "aa", "p": "pp", "g": "gq"}
     cnt = {"v": 0, "a": 0, "p": 0, "g": 0}
@@ -169,6 +171,13 @@ def rank_program(g, core, T, topo):
     def at(s, d):
         return s if s < d else s - 1
 
+    def load_w(e, h):
+        dma(e, "dw%d" % h, 16, [], ["wt%d" % h], T.wt[:, 2048 * h:2048 * h + 2048], T.w[:, 2048 * h:2048 * h + 2048])
+
+    def pack(h):
+        w = slice(512 * h, 512 * h + 512)
+        op("v", g.vector.quantize_mx, ["wt%d" % h], ["wq%d" % h], T.wq[:, w], T.wqs[:, w], T.wt[:, 2048 * h:2048 * h + 2048])
+
     dma("y", "dsrc", 128, [], ["src"], T.src[0:64, :], T.alt[:, :])
     dma("y", "dsrc", 128, [], ["src"], T.src[64:128, 0:1], T.f1[:, :])
     dma("y", "dsrc", 128, [], ["src"], T.src[64:128, 1:2], T.f2[:, :])
@@ -222,23 +231,20 @@ def rank_program(g, core, T, topo):
     need("g", wr["sv"])
     spread("aL", lambda d: (b("sv"), T.lists[me]))
     dma("y", "down", 16, ["sv"], ["lown"], T.lists[me], b("sv"))
+    load_w("y", 0)
 
     op("g", g.partition_broadcast, ["row"], ["rowb"], T.rowb[0:32, :], T.row[0:1, :], 32)
     iota("jn", b("jn"), [[0, 10], [1, 32]], 0, 0, False)
     for r1, k in ((128, 4), (16, 0)):
-        iota("val0", b("val0", 0, r1), [[8, 2], [1, 4], [16, 4]], Z + P + k, 0)
+        iota("val0", b("val0", 0, r1), [[8, 2], [1, 4], [16, 4]], SM + Z + P + k, 0)
     iota("de", b("de"), [[16, 32]], CH, 1, False)
     iota("gli", b("gli"), [[16, 20]], 0, 1, False)
     iota("gli", b("gli", 0, 16), [[16, 20]], OB, 1, False)
+    iota("df0", b("df0"), [[0, 8]], E0 * me, 1)
     for r1, k in ((128, 4), (16, 0)):
-        iota("val.c", b("val", 0, r1, 0, 128), [[2, 8], [16, 16]], Z + k // 4, 0)
-        iota("val.v", b("val", 0, r1, 128, 160), [[8, 2], [1, 4], [16, 4]], Z + P + k, 0)
-    iota("df", b("df"), [[16, 32]], 0, 1)
-    for nm, w in (("ch0", 1), ("ch1", 3)):
-        if me > 0:
-            iota(nm, T[nm][:, 0:w * me], [[IDS, me], [0, w]], S0 + ID0 - Z, 0)
-        if me < N - 1:
-            iota(nm, T[nm][:, w * me:w * (N - 1)], [[IDS, N - 1 - me], [0, w]], S0 + ID0 - Z + IDS * (me + 1), 0)
+        iota("val.c", b("val", 0, r1, 0, 128), [[2, 8], [16, 16]], SM + Z + k // 4, 0)
+        iota("val.v", b("val", 0, r1, 128, 160), [[8, 2], [1, 4], [16, 4]], SM + Z + P + k, 0)
+    iota("df1", b("df1", 0, 128, 0, 21), [[0, N - 1], [16, 3]], E1 * me, 1)
     iota("slot.own", b("slot", 0, 128, S0 + ID0 + IDS * me, S0 + ID0 + IDS * me + IDS), [[1, IDS]], Z, 0)
     iota("sl0", b("sl0"), [[1, (N - 1) * E0]], OWN, 0)
     iota("sl1", b("sl1"), [[1, (N - 1) * E1]], W1, 0)
@@ -275,21 +281,20 @@ def rank_program(g, core, T, topo):
         tt(["pf", key], ["qq"], s("qq", n), s("pf", n), marks, A.mult)
         op("v", g.vector.transpose, ["qq"], ["tq"], s("tq", n), s("qq", n))
         scan(["tq", "k32"], ["ts"], s("ts", n), s("k32", n), s("tq", n), 0.0)
-        copy(["ts"], ["ri"], s("ri"), T.ts[0:32, 31:n:32])
-        tsc(["ri"], ["lo"], s("lo"), s("ri"), 15, A.bitwise_and)
-        tsc(["ri"], ["hi"], s("hi"), s("ri"), 4, A.arith_shift_right)
-        tsc(["lo"], ["l2"], s("l2"), s("lo"), float(width), A.mult)
-        tt(["l2", "hi"], ["sm2"], s("sm2"), s("l2"), s("hi"), A.add)
+        u = T.ts[0:32, 31:n:32]
+        tsc(["ts"], ["hi"], s("hi"), u, 1.0 / 16, A.mult, -0.46875, A.add)
+        tsc(["ts"], ["lo"], s("lo"), u, float(width), A.mult)
+        tsc(["hi"], ["l2"], s("l2"), s("hi"), 1.0 - 16.0 * width, A.mult)
+        tt(["l2", "lo"], ["sm2"], s("sm2"), s("l2"), s("lo"), A.add)
         tt(["sm2", "dd"], ["mx2"], s("mx2"), s("sm2"), s("dd"), A.max)
         copy(["mx2"], [of], s(of), s("mx2"))
         copy([of] + vkeys, [pl], T[pl][:, :].indirect(T[of][:, 0:k]), T[val][:, :])
 
     compact(V, T.md[0:32, IT:RS], "md", "b16", C0, "ofp0", "val0", ["val0"], "pl0")
-    for nm, r0 in (("la0", 0), ("lb0", 16)):
-        dma("g", "dpl0", 32, ["pl0"], [nm], b(nm), T.pl0[r0:r0 + 8, K0:K0 + 16 * C0])
     tt(["hb"], ["ne2"], b("ne2", 0, 32), T.hb[0:32, P:IT], T.hb[0:32, IT:RS], A.not_equal)
     tt(["ne2", "md"], ["md"], T.md[0:32, P:IT], T.md[0:32, P:IT], b("ne2", 0, 32), A.mult)
     copy(["gli"], ["gl"], T.gl[:, 0:16], T.gli[:, 0:16])
+    pack(0)
 
     arrive("aL", "lfar")
     for e, half in (("y", 0), ("a", 1)):
@@ -299,8 +304,9 @@ def rank_program(g, core, T, topo):
             dma(e, "df1", 128, ["lfar", "lown"], ["f1o"], T.f1f[0:16, 4 * h:4 * h + 4], T.lists[h, 64:96, 2:4])
         for p in range(8 * half, 8 * half + 8):
             dma(e, "dvf", 256, ["lfar", "lown"], ["vf"], T.vf[p:p + 1, :], T.lists[:, 64:128, :])
-    dma("y", "dw0", 16, [], ["wt0"], T.wt[:, 0:2048], T.w[:, 0:2048])
-    dma("a", "dw1", 16, [], ["wt1"], T.wt[:, 2048:4096], T.w[:, 2048:4096])
+    for nm, r0 in (("la0", 0), ("lb0", 16)):
+        dma("y", "dpl0", 32, ["pl0"], [nm], b(nm), T.pl0[r0:r0 + 8, K0:K0 + 16 * C0])
+    load_w("y", 1)
 
     def look(table, keys, of, ok, gm, gk, n):
         tt(keys + [ok, "mask"], [gk], gm, table.indirect(of), T.mask[:, 0:n], A.mult)
@@ -311,6 +317,28 @@ def rank_program(g, core, T, topo):
         sb("wn", "wi", 4095, A.bitwise_and)
         tb("wm", "wn", dump, A.max)
         copy(["wm"], [of], b(of), b("wm"))
+
+    def picks(k, first, e):
+        la, lb, ls, pku, dst, dss, meta, mt = [x + k for x in ("la", "lb", "ls", "pk", "sn", "sn", "meta", "mt")]
+        pku, dss, mtu, w = pku + "u", dss + "s", mt + "u", W[k]
+        n = w * (N - 1)
+        tb(ls, la, lb, A.add)
+        tsc([ls], [pku], b(pku), b(ls), -float(SM), A.add, 0.0, A.max)
+        tt([ls, "df" + k], [mt], b(mt, 0, 128, 0, n), b(ls, 0, 128, 0, n), b("df" + k, 0, 128, 0, n), A.max)
+        copy([mt], [mtu], b(mtu, 0, 128, 0, n), b(mt, 0, 128, 0, n))
+        copy(["qo.own", pku], [dst], b(dst).bitcast(dt.uint32), b("qo").bitcast(dt.uint32).indirect(b(pku)))
+        copy(["qo.own", pku], [dss], b(dss), b("qos").indirect(b(pku)), "a")
+        need("g", wr[mtu])
+        spread("aM" + k, lambda d: (T[mtu][:, w * at(d, me):w * at(d, me) + w], T[meta][:, w * at(me, d):w * at(me, d) + w]))
+        need("g", wr[dst])
+        spread("aC" + k, lambda d: (T[dst][:, e * at(d, me):e * at(d, me) + e].bitcast(dt.uint8),
+                                    T.fw[:, first + e * at(me, d):first + e * at(me, d) + e].bitcast(dt.uint8)))
+        need("g", wr[dss])
+        spread("aS" + k, lambda d: (T[dss][:, e * at(d, me):e * at(d, me) + e],
+                                    T.fws[:, first + e * at(me, d):first + e * at(me, d) + e]))
+        arrive("aM" + k, meta)
+        arrive("aC" + k, "fw" + k)
+        arrive("aS" + k, "fws" + k)
 
     X = ["xt", "xt.d"]
     tab = T.xt[:, :]
@@ -328,111 +356,82 @@ def rank_program(g, core, T, topo):
     diag("ofz", "de")
     copy(["vf", "ofq"], X, tab.indirect(b("ofq")), v2)
     copy(X + ["ofz"], ["old2"], b("old2"), tab.indirect(b("ofz")), "a")
-    copy(["xt"], ["x2s"], T.x2s[0:16, :], OX, "a")
-
-    def picks(k, first, e, w):
-        la, lb, ls, pku, dst, dss, meta = [x + k for x in ("la", "lb", "ls", "pk", "sn", "sn", "meta")]
-        pku, dss = pku + "u", dss + "s"
-        tb(ls, la, lb, A.add)
-        copy([ls], [pku], b(pku), b(ls))
-        copy(["qo.own", pku], [dst], b(dst).bitcast(dt.uint32), b("qo").bitcast(dt.uint32).indirect(b(pku)))
-        copy(["qo.own", pku], [dss], b(dss), b("qos").indirect(b(pku)), "a")
-        need("g", wr[pku])
-        spread("aM" + k, lambda d: (T[pku][:, w * at(d, me):w * at(d, me) + w], T[meta][:, w * at(me, d):w * at(me, d) + w]))
-        need("g", wr[dst])
-        spread("aC" + k, lambda d: (T[dst][:, e * at(d, me):e * at(d, me) + e].bitcast(dt.uint8),
-                                    T.fw[:, first + e * at(me, d):first + e * at(me, d) + e].bitcast(dt.uint8)))
-        need("g", wr[dss])
-        spread("aS" + k, lambda d: (T[dss][:, e * at(d, me):e * at(d, me) + e],
-                                    T.fws[:, first + e * at(me, d):first + e * at(me, d) + e]))
-        arrive("aM" + k, meta)
-        arrive("aC" + k, "fw" + k)
-        arrive("aS" + k, "fws" + k)
-
-    picks("0", OWN, E0, 1)
+    copy(["xt"], ["x2s"], T.x2s[0:16, :], OX)
     copy(["of1"], ["gl.v"], T.gl[:, 16:20], T.of1[:, 4 * me:4 * me + 4])
-    for h in range(2):
-        w = slice(512 * h, 512 * h + 512)
-        op("v", g.vector.quantize_mx, ["wt%d" % h], ["wq%d" % h], T.wq[:, w], T.wqs[:, w], T.wt[:, 2048 * h:2048 * h + 2048])
+    picks("0", OWN, E0)
     copy(["old1", "ofz"], X, tab.indirect(b("ofz")), b("old1"))
 
     tt(X + ["gl", "gl.v", "a0", "a0v"], ["ei"], b("ei"), tab.indirect(b("gl")), b("a0"), A.not_equal)
     tt(["ei", "md"], ["gg"], T.gg[0:32, :], T.ei[0:32, :], T.md[0:32, 0:IT], A.mult)
     compact(IT, T.gg[0:32, :], "gg", "b48", C1, "ofp", "val", ["val.c", "val.v"], "pl1")
+    for t, nm in enumerate(("x1s", "x2s")):
+        dma("y", "di%d" % t, 16, [nm], ["idw%d" % t], T.idw[:, 16 * t:16 * t + 16], T[nm][0:8, :])
     for nm, r0 in (("la1", 0), ("lb1", 16)):
         dma("y", "dpl1", 32, ["pl1"], [nm], b(nm), T.pl1[r0:r0 + 8, K1:K1 + 16 * C1])
-
     copy(["xt"], ["x3s"], T.x3s[0:16, :], OX, "a")
-    tb("gm", "old2", "mask", A.mult)
-    diag("ofw", "dd")
-    for t in range(3):
-        nm = "x%ds" % (t + 1)
-        dma("y", "di%d" % t, 16, [nm], ["idw%d" % t], T.idw[:, 16 * t:16 * t + 16], T[nm][0:8, :])
+    dma("y", "di2", 16, ["x3s"], ["idw2"], T.idw[:, 32:48], T.x3s[0:8, :])
 
-    picks("1", W1, E1, 3)
-
-    def fill_slots(k, n):
-        meta, chn, of, vals = "meta" + k, "ch" + k, "ofs" + k, "sl" + k
-
-        def s(name):
-            return b(name, 0, 128, 0, n)
-        copy([meta], ["m1"], s("m1"), s(meta))
-        tsc(["m1"], ["m2"], s("m2"), s("m1"), 1.0, A.min)
-        tt(["m2", chn], ["m3"], s("m3"), s("m2"), s(chn), A.mult)
-        tt(["m3", "m1"], ["m4"], s("m4"), s("m3"), s("m1"), A.add)
-        tt(["m4", "df"], ["m5"], s("m5"), s("m4"), s("df"), A.max)
-        copy(["m5"], [of], s(of), s("m5"))
-        copy([of, vals], ["slot", "slot.own", "slot.z"], b("slot").indirect(s(of)), b(vals))
+    def fill_slots(k):
+        copy(["meta" + k, "sl" + k], ["slot", "slot.own", "slot.z"],
+             b("slot").indirect(T["meta" + k][:, 0:W[k] * (N - 1)]), b("sl" + k))
 
     def slots(keys, c0, c1):
-        i, s = "idi%d" % c0, "ids%d" % c0
-        copy(keys, [i], b("idi", 0, 128, c0, c1), T.idw[:, c0:c1])
-        tsc([i], [s], b("ids", 0, 128, c0, c1), b("idi", 0, 128, c0, c1), 12, A.arith_shift_right)
-        tsc([s], ["idu%d" % c0], T.idu[:, c0:c1], b("ids", 0, 128, c0, c1), float(S0), A.add)
+        k = "ids%d" % c0
+        tsc(keys, [k], b("ids", 0, 128, c0, c1), T.idw[:, c0:c1], 1.0 / 4096, A.mult, S0 - 0.375, A.add)
+        copy([k], ["idu%d" % c0], T.idu[:, c0:c1], b("ids", 0, 128, c0, c1))
 
-    def stand(t, key):
-        gk, w = "gs%d" % t, slice(P * t, P * t + P)
-        look(b("slot"), ["slot", "slot.own", "slot.z"], T.idu[:, 16 * t:16 * t + 16], key, T.gs[:, w], gk, P)
-        scan([gk, "keep"], [gk + "c"], T.gsc[:, w], T.keep[:, 0:P], T.gs[:, w], 0.0)
-        copy([gk + "c"], ["so%d" % t], T.so[:, 16 * t:16 * t + 16], T.gsc[:, P * t + 15:P * t + P:16])
+    def stand(c0, c1):
+        gk, w, n = "gs%d" % c0, slice(16 * c0, 16 * c1), 16 * (c1 - c0)
+        look(b("slot"), ["slot", "slot.own", "slot.z"], T.idu[:, c0:c1], "idu%d" % c0, T.gs[:, w], gk, n)
+        scan([gk, "keep"], [gk + "c"], T.gsc[:, w], T.keep[:, 0:n], T.gs[:, w], 0.0)
+        op("v", g.vector.tensor_copy, [gk + "c"], ["so%d" % t for t in range(c0 // 16, c1 // 16)], T.so[:, c0:c1],
+           T.gsc[:, 16 * c0 + 15:16 * c1:16])
 
     def place(t):
-        n = W1 if t == 0 else WW
-        u = T.so[:, 16 * t:16 * t + 16]
-        pk, ps, ks = "pk%d" % t, "ps%d" % t, (["0"] if t == 0 else ["0", "1"])
-        copy(["fw.own", "so%d" % t] + ["fw" + k for k in ks], [pk], b(pk).bitcast(dt.uint32),
-             T.fw[:, 0:n].bitcast(dt.uint32).indirect(u))
-        copy(["fw.own", "so%d" % t] + ["fws" + k for k in ks], [ps], b(ps), T.fws[:, 0:n].indirect(u), "a")
+        copy(["fw.own", "so%d" % t] + ["fw%d" % k for k in range(min(t, 1) + 1)], ["pk%d" % t], b("pk%d" % t).bitcast(dt.uint32),
+             T.fw[:, 0:WW if t else W1].bitcast(dt.uint32).indirect(T.so[:, 16 * t:16 * t + 16]))
+
+    def products(t):
+        pk, ps = "pk%d" % t, "ps%d" % t
+        copy(["fw.own", "so%d" % t] + ["fws%d" % k for k in range(min(t, 1) + 1)], [ps], b(ps),
+             T.fws[:, 0:WW if t else W1].indirect(T.so[:, 16 * t:16 * t + 16]), "a")
         for i in range(O * t, O * t + O):
             w = slice(128 * i, 128 * i + 128)
             op("p", g.tensor.matmul_mx, ["wq%d" % (i // 4), pk, ps], ["acc%d" % i], T.acc[:, 512 * i:512 * i + P],
                T.wq[:, w], T.wqs[:, w], b(pk), b(ps), True, True)
 
-    def out(t):
+    def out(t, es):
         for o in range(O):
             i = O * t + o
             w = slice(P * i, P * i + P)
-            copy(["acc%d" % i], ["ys%d" % i], T.ys[:, w], T.acc[:, 512 * i:512 * i + P], "va"[o])
+            copy(["acc%d" % i], ["ys%d" % i], T.ys[:, w], T.acc[:, 512 * i:512 * i + P], es[o])
             dma("y", "dy", 16 * R * O, ["ys%d" % i], ["y%d" % i], T.y[:, w], T.ys[:, w])
 
+    fill_slots("0")
+    slots(["idw0"], 0, 16)
+    stand(0, 16)
+    pack(1)
+    picks("1", W1, E1)
+    place(0)
+    products(0)
+    out(0, "aa")
+    tb("gm", "old2", "mask", A.mult)
+    diag("ofw", "dd")
     copy(["old2", "ofw"], X, tab.indirect(b("ofw")), b("old2"))
     dma("y", "di3", 16, ["xt"], ["idw3"], T.idw[:, 48:64], T.xt[0:8, OB:OB + P])
-    fill_slots("0", N - 1)
-    slots(["idw0"], 0, 16)
-    stand(0, "idu0")
-    place(0)
-    out(0)
     slots(["idw1", "idw2"], 16, 48)
-    fill_slots("1", 3 * (N - 1))
-    stand(1, "idu16")
-    stand(2, "idu16")
+    fill_slots("1")
+    stand(16, 48)
     place(1)
-    slots(["idw3"], 48, 64)
-    stand(3, "idu48")
     place(2)
-    out(1)
+    products(1)
+    products(2)
+    out(1, "aa")
+    slots(["idw3"], 48, 64)
+    stand(48, 64)
     place(3)
-    out(2)
-    out(3)
+    products(3)
+    out(2, "va")
+    out(3, "va")
     need("y", [("dy", 16 * R * O)])
     need("g", [("lsent", sent[0])])

@@ -16,7 +16,7 @@ W1 = OWN + (N - 1) * E0
 WW = W1 + (N - 1) * E1
 IT = P + V
 K0, K1 = 64, 200
-C0, C1 = 8, 22
+C0, C1 = 7, 21
 W = {"0": 1, "1": 3}
 
 SCRATCH = {"lists": ("dram", [8, 128, 4], "float32"), "acc": ("psum", [128, 4096], "float32")}
@@ -37,21 +37,21 @@ def _pool(buf, dtype, **cols):
     SCRATCH[buf] = ("sbuf", [128, a], dtype)
 
 
-_sb("int32", src=4, pi=1, row=RS, rowb=RS, hb=RS, jm=CH, jn=IT, dd=32, de=32, gli=20)
-_sb("float32", sv=4, e16=4, md=RS, mask=CH, keep=CH, gm=CH, scn=CH, old1=CH, old2=CH, ones=IT, k32=IT, df0=8, df1=22, f1f=32,
+_sb("int32", src=4, pi=1, rowb=RS, hb=RS, dd=32, de=32, gli=20)
+_sb("float32", sv=4, e16=4, jm=16, gm=CH, scn=CH, old1=CH, old2=CH, f1f=32,
     vf=4 * CH, xt=XW, a0=IT, x1s=P, x2s=P, x3s=P, ei=IT, gg=IT, pf=IT, qq=IT, tq=IT, ts=IT, val=160, val0=32, pl0=208,
     pl1=560, la0=C0, lb0=C0, la1=C1, lb1=C1, slot=S0 + ID0 + N * IDS + 24, sl0=(N - 1) * E0, sl1=(N - 1) * E1,
-    idw=64, gs=4 * P, gsc=4 * P, ys=2048)
-_sb("uint16", of1=32, ofq=32, ofz=32, ofw=32, gl=20, ofp=10, ofp0=2, pk0u=C0, pk1u=C1, mt0u=8, mt1u=22, meta0=8, meta1=22, idu=64,
+    idw=64, gs=4 * P, gsc=4 * P, ys=2048, dcol=1, b16=1, b48=1)
+_sb("uint16", of1=32, ofq=32, ofz=32, ofw=32, gl=20, ofp=10, ofp0=2, pk0u=C0, pk1u=C1, mt0u=C0, mt1u=C1, meta0=C0, meta1=C1, idu=64,
     so=64)
-_sb("bfloat16", cv=4 * OWN, wt=4096)
-_sb("float8_e4m3fn_x4", wq=1024, qo=OWN, sn0=128, sn1=352, fw=WW, pk0=P, pk1=P, pk2=P, pk3=P)
-_sb("uint8", wqs=1024, qos=OWN, sn0s=128, sn1s=352, fws=WW, ps0=P, ps1=P, ps2=P, ps3=P)
-_pool("tf", "float32", sxx=4, sxh=4, k2=4, k2a=4, sa=4, sb=4, sc=4, s1=4, s2=4, s3=4, sm=4, pif=1, c64=1, cm=1, c16=1, ck=1, pmf=1,
-      dc1=1, dcol=1, bg=1, h16=1, h48=1, b16=1, b48=1, ne2=V, ls0=C0, ls1=C1, mt0=8, mt1=22)
+_sb("bfloat16", cv=4 * OWN, wt=4096, ones=IT, k32=IT, md=RS, mask=CH, keep=CH)
+_sb("float8_e4m3fn_x4", wq=1024, qo=OWN, sn0=112, sn1=336, fw=WW, pk0=P, pk1=P, pk2=P, pk3=P)
+_sb("uint8", wqs=1024, qos=OWN, sn0s=112, sn1s=336, fws=WW, ps0=P, ps1=P, ps2=P, ps3=P)
+_pool("tf", "float32", sxx=4, sxh=4, k2=4, k2a=4, sa=4, sb=4, sc=4, s1=4, s2=4, s3=4, sm=4, c64=1, cm=1, c16=1, ck=1, pmf=1,
+      ne2=V, mt0=C0, mt1=C1)
 _pool("ti", "int32", sy=4, shh=4, pa3=1, pa2=1, pm=1, lo=10, hi=10, l2=10, sm2=10, mx2=10, wi=32, wn=32, wm=32, ids=64)
 SEMAPHORES = ["vv", "aa", "pp", "gq", "lsent", "aL", "aM0", "aC0", "aS0", "aM1", "aC1", "aS1", "dsrc", "drow", "dcv", "dw0", "dw1",
-              "down", "dfan", "df1", "dvf", "dpl0", "dpl1", "di0", "di1", "di2", "di3", "dy"]
+              "dfw", "down", "dfan", "df1", "dvf", "dpl0", "dpl1", "di0", "di1", "di2", "di3", "dy"]
 
 
 def rank_program(g, core, T, topo):
@@ -184,19 +184,28 @@ def rank_program(g, core, T, topo):
     for c in range(4):
         dma("a", "dsrc", 128, [], ["src"], T.src[64 + c // 2:96:2, 2 + c % 2:3 + c % 2], T.f1[4 * c:4 * c + 4, :])
     dma("y", "dsrc", 128, [], ["src"], T.src[96:128, 2:4], T.f1[:, :])
-    dma("a", "drow", 48, [], ["row"], T.row[0:1, 0:P], T.alt[:, :])
-    dma("a", "drow", 48, [], ["row"], T.row[0:1, P:IT], T.f2[:, :])
-    dma("a", "drow", 48, [], ["row"], T.row[0:1, IT:RS], T.f1[:, :])
+    for p in range(N):
+        for lo, t in ((0, T.alt), (P, T.f2), (IT, T.f1)):
+            dma("ya"[p % 2], "drow", 16 * 3 * N, [], ["rowb"], T.rowb[p:p + 1, lo:lo + (P if lo == 0 else V)], t[:, :])
     dma("y", "dcv", 32, [], ["cv.c"], T.cv[:, 4 * Z:4 * (Z + P)], T.c[:, :])
     dma("y", "dcv", 32, [], ["cv.c"], T.cv[:, 4 * (Z + P):4 * OWN], T.v[:, :])
 
     iota("pi", b("pi"), [[1, 1]], 0, 1, False)
     iota("e16", b("e16"), [[16, 4]], 0, 0)
     iota("dd", b("dd"), [[16, 32]], 0, 1, False)
+    iota("jm", b("jm"), [[1, 16]], 0, 0)
     iota("f1o", b("f1f"), [[16, 32]], 0, 1)
-    iota("jm", b("jm"), [[0, 32], [1, 16]], 0, 0, False)
+    iota("dcol", b("dcol"), [[1, 1]], 0, 1)
+    iota("dcol", b("dcol", 0, me + 1), [[1, 1]], 99, 0)
+    if me:
+        iota("dcol", b("dcol", 0, me), [[1, 1]], 0, 1)
 
-    fill("xt.d", T.xt[:, 0:D0 + 128], 0.0)
+    def begin(nm, e, k):
+        iota(nm, b(nm), [[1, 1]], 16 * k - 1 - e, e)
+        iota(nm, b(nm, 0, me + 1), [[1, 1]], 16 * k - 1, e)
+
+    begin("b16", E0, K0)
+    fill("md", T.md[0:32, :], 0.0)
     own0 = float(ID0 + IDS * me)
     sb("pa3", "pi", 3, A.bitwise_and)
     sb("pa2", "pi", 2, A.arith_shift_right)
@@ -213,10 +222,6 @@ def rank_program(g, core, T, topo):
     tsc(["e16", "cm"], ["k2a"], b("k2a", 0, 64), b("e16", 0, 64), b("cm", 0, 64), A.add, 4096.0, A.mult)
     tsc(["ck"], ["k2"], b("k2", 64, 128, 1, 2), b("ck", 64), 4096.0, A.mult, D0 + 4096.0 * (own0 + P - 16), A.add)
     tsc(["k2a"], ["k2"], b("k2", 0, 64), b("k2a", 0, 64), D0 + 4096.0 * own0, A.add)
-    for k in range(2):
-        copy(["xt.d"], ["vf"], T.vf[:, D0 * k:D0 * k + D0], T.xt[:, 0:D0], "a")
-    copy(["xt.d"], ["a0"], b("a0"), T.xt[:, 0:IT], "a")
-    copy(["xt.d"], ["pl1"], b("pl1"), T.xt[:, 0:560], "a")
 
     sb("sy", "src", 4, A.arith_shift_right)
     sb("shh", "src", 8, A.arith_shift_right)
@@ -233,44 +238,37 @@ def rank_program(g, core, T, topo):
     dma("y", "down", 16, ["sv"], ["lown"], T.lists[me], b("sv"))
     load_w("y", 0)
 
-    op("g", g.partition_broadcast, ["row"], ["rowb"], T.rowb[0:32, :], T.row[0:1, :], 32)
-    iota("jn", b("jn"), [[0, 10], [1, 32]], 0, 0, False)
+    fill("xt.z", T.xt[:, 0:CH], 0.0)
+    copy(["xt.z"], ["xt.d"], T.xt[:, CH:2 * CH], T.xt[:, 0:CH], "a")
+    copy(["xt.z"], ["xt.d"], T.xt[:, D0:D0 + 128], T.xt[:, 0:128], "a")
+    for k in range(2):
+        copy(["xt.z"], ["vf"], T.vf[:, k:4 * CH:4], T.xt[:, 0:CH], "a")
+
+    fill("pl0", b("pl0", 0, 32, K0, K0 + 16 * C0), 0.0)
     for r1, k in ((128, 4), (16, 0)):
         iota("val0", b("val0", 0, r1), [[8, 2], [1, 4], [16, 4]], SM + Z + P + k, 0)
-    iota("de", b("de"), [[16, 32]], CH, 1, False)
+    iota("pl0", b("pl0", 0, 16, K0, K0 + 16 * C0), [[1, 16], [0, N - 1]], E0 * me, 0)
     iota("gli", b("gli"), [[16, 20]], 0, 1, False)
     iota("gli", b("gli", 0, 16), [[16, 20]], OB, 1, False)
-    iota("df0", b("df0"), [[0, 8]], E0 * me, 1)
+    iota("de", b("de"), [[16, 32]], CH, 1, False)
+    begin("b48", E1, K1)
+    iota("pl1", b("pl1", 0, 32, K1, K1 + 16 * C1), [[0, 16 * C1]], 0, 0)
+    iota("pl1", b("pl1", 0, 16, K1, K1 + 16 * C1), [[1, 16], [0, N - 1], [16, 3]], E1 * me, 0)
     for r1, k in ((128, 4), (16, 0)):
         iota("val.c", b("val", 0, r1, 0, 128), [[2, 8], [16, 16]], SM + Z + k // 4, 0)
         iota("val.v", b("val", 0, r1, 128, 160), [[8, 2], [1, 4], [16, 4]], SM + Z + P + k, 0)
-    iota("df1", b("df1", 0, 128, 0, 21), [[0, N - 1], [16, 3]], E1 * me, 1)
-    iota("slot.own", b("slot", 0, 128, S0 + ID0 + IDS * me, S0 + ID0 + IDS * me + IDS), [[1, IDS]], Z, 0)
-    iota("sl0", b("sl0"), [[1, (N - 1) * E0]], OWN, 0)
-    iota("sl1", b("sl1"), [[1, (N - 1) * E1]], W1, 0)
 
-    fill("cv.z", T.cv[:, 0:4 * Z], 0.0)
     fill("ones", b("ones"), 1.0)
-    fill("pl0", b("pl0"), 0.0)
-    fill("slot.z", T.slot[:, S0:S0 + ID0], 0.0)
-    copy(["pi"], ["pif"], b("pif"), b("pi"))
-    sb("dc1", "pif", float(me), A.is_equal, 99.0, A.mult)
-    tb("dcol", "dc1", "pif", A.add)
-    sb("bg", "pif", float(me), A.is_gt)
-    for nm, hh, e, k in (("b16", "h16", E0, K0), ("b48", "h48", E1, K1)):
-        tb(hh, "pif", "bg", A.subtract)
-        sb(nm, hh, float(e), A.mult, 16.0 * k - 1.0, A.add)
+    fill("k32", b("k32"), 1.0)
+    fill("k32", T.k32[:, 0:IT:32], 0.0)
+    tsc(["rowb"], ["hb"], T.hb[0:N, :], T.rowb[0:N, :], 8, A.arith_shift_right)
+    tsc(["hb", "dcol"], ["md"], T.md[0:N, :], T.hb[0:N, :], b("dcol", 0, N), A.is_equal)
     copy(["dd"], ["ofp0"], b("ofp0"), T.dd[:, 0:2])
     copy(["dd"], ["ofp"], b("ofp"), T.dd[:, 0:10])
     sb("pm", "pi", 15, A.bitwise_and)
+    fill("cv.z", T.cv[:, 0:4 * Z], 0.0)
     copy(["pm"], ["pmf"], b("pmf"), b("pm"))
-    tsc(["jm", "pmf"], ["mask"], b("mask"), b("jm"), b("pmf"), A.is_equal)
-    sb("keep", "jm", 0.0, A.is_gt)
-    for dst, sc in (("qo", "qos"), ("fw", "fws")):
-        op("v", g.vector.quantize_mx, ["cv.z", "cv.c"], [dst + ".own"], T[dst][:, 0:OWN], T[sc][:, 0:OWN], T.cv[:, :])
-    sb("k32", "jn", 0.0, A.is_gt)
-    tsc(["rowb"], ["hb"], T.hb[0:32, :], T.rowb[0:32, :], 8, A.arith_shift_right)
-    tsc(["hb", "dcol"], ["md"], T.md[0:32, :], T.hb[0:32, :], b("dcol", 0, 32), A.is_equal)
+    op("v", g.vector.quantize_mx, ["cv.z", "cv.c"], ["qo.own"], T.qo[:, 0:OWN], T.qos[:, 0:OWN], T.cv[:, :])
 
     def compact(n, marks, key, base, width, of, val, vkeys, pl):
         k = n // 32
@@ -291,22 +289,32 @@ def rank_program(g, core, T, topo):
         copy([of] + vkeys, [pl], T[pl][:, :].indirect(T[of][:, 0:k]), T[val][:, :])
 
     compact(V, T.md[0:32, IT:RS], "md", "b16", C0, "ofp0", "val0", ["val0"], "pl0")
-    tt(["hb"], ["ne2"], b("ne2", 0, 32), T.hb[0:32, P:IT], T.hb[0:32, IT:RS], A.not_equal)
-    tt(["ne2", "md"], ["md"], T.md[0:32, P:IT], T.md[0:32, P:IT], b("ne2", 0, 32), A.mult)
+    tt(["hb"], ["ne2"], b("ne2", 0, N), T.hb[0:N, P:IT], T.hb[0:N, IT:RS], A.not_equal)
+    tt(["ne2", "md"], ["md"], T.md[0:N, P:IT], T.md[0:N, P:IT], b("ne2", 0, N), A.mult)
+    fill("keep", b("keep"), 1.0)
+    fill("keep", T.keep[:, 0:CH:16], 0.0)
+    tsc(["jm", "pmf"], ["mask"], T.mask[:, 0:16], b("jm"), b("pmf"), A.is_equal)
+    n = 16
+    while n < CH:
+        copy(["mask"], ["mask"], T.mask[:, n:2 * n], T.mask[:, 0:n])
+        n *= 2
+    fill("slot.z", T.slot[:, S0:S0 + ID0], 0.0)
     copy(["gli"], ["gl"], T.gl[:, 0:16], T.gli[:, 0:16])
-    pack(0)
 
     arrive("aL", "lfar")
     for e, half in (("y", 0), ("a", 1)):
         for p in range(8 * half, 8 * half + 8):
-            dma(e, "dfan", 256, ["lfar", "lown"], ["xt", "xt.d"], T.xt[p:p + 1, D0:XW], T.lists[:, 0:64, :])
+            dma(e, "dfan", 256, ["lfar", "lown"], ["xt", "xt.d", "xt.z"], T.xt[p:p + 1, D0:XW], T.lists[:, 0:64, :])
         for h in range(4 * half, 4 * half + 4):
             dma(e, "df1", 128, ["lfar", "lown"], ["f1o"], T.f1f[0:16, 4 * h:4 * h + 4], T.lists[h, 64:96, 2:4])
         for p in range(8 * half, 8 * half + 8):
             dma(e, "dvf", 256, ["lfar", "lown"], ["vf"], T.vf[p:p + 1, :], T.lists[:, 64:128, :])
+    copy(["xt.z"], ["a0"], b("a0"), T.xt[:, 0:IT], "a")
     for nm, r0 in (("la0", 0), ("lb0", 16)):
         dma("y", "dpl0", 32, ["pl0"], [nm], b(nm), T.pl0[r0:r0 + 8, K0:K0 + 16 * C0])
     load_w("y", 1)
+    dma("y", "dfw", 32, ["qo.own"], ["fw.own"], T.fw[:, 0:OWN].bitcast(dt.uint8), T.qo[:, 0:OWN].bitcast(dt.uint8))
+    dma("y", "dfw", 32, ["qo.own"], ["fw.own"], T.fws[:, 0:OWN], T.qos[:, 0:OWN])
 
     def look(table, keys, of, ok, gm, gk, n):
         tt(keys + [ok, "mask"], [gk], gm, table.indirect(of), T.mask[:, 0:n], A.mult)
@@ -319,13 +327,11 @@ def rank_program(g, core, T, topo):
         copy(["wm"], [of], b(of), b("wm"))
 
     def picks(k, first, e):
-        la, lb, ls, pku, dst, dss, meta, mt = [x + k for x in ("la", "lb", "ls", "pk", "sn", "sn", "meta", "mt")]
+        la, lb, pku, dst, dss, meta, mt = [x + k for x in ("la", "lb", "pk", "sn", "sn", "meta", "mt")]
         pku, dss, mtu, w = pku + "u", dss + "s", mt + "u", W[k]
-        n = w * (N - 1)
-        tb(ls, la, lb, A.add)
-        tsc([ls], [pku], b(pku), b(ls), -float(SM), A.add, 0.0, A.max)
-        tt([ls, "df" + k], [mt], b(mt, 0, 128, 0, n), b(ls, 0, 128, 0, n), b("df" + k, 0, 128, 0, n), A.max)
-        copy([mt], [mtu], b(mtu, 0, 128, 0, n), b(mt, 0, 128, 0, n))
+        tb(mt, la, lb, A.max)
+        tsc([mt], [pku], b(pku), b(mt), -float(SM), A.add, 0.0, A.max)
+        copy([mt], [mtu], b(mtu), b(mt))
         copy(["qo.own", pku], [dst], b(dst).bitcast(dt.uint32), b("qo").bitcast(dt.uint32).indirect(b(pku)))
         copy(["qo.own", pku], [dss], b(dss), b("qos").indirect(b(pku)), "a")
         need("g", wr[mtu])
@@ -340,7 +346,7 @@ def rank_program(g, core, T, topo):
         arrive("aC" + k, "fw" + k)
         arrive("aS" + k, "fws" + k)
 
-    X = ["xt", "xt.d"]
+    X = ["xt", "xt.d", "xt.z"]
     tab = T.xt[:, :]
     OX = T.xt[0:16, OB:OB + P]
     v2, v1 = T.vf[:, 0:4 * CH:4], T.vf[:, 1:4 * CH:4]
@@ -356,9 +362,13 @@ def rank_program(g, core, T, topo):
     diag("ofz", "de")
     copy(["vf", "ofq"], X, tab.indirect(b("ofq")), v2)
     copy(X + ["ofz"], ["old2"], b("old2"), tab.indirect(b("ofz")), "a")
-    copy(["xt"], ["x2s"], T.x2s[0:16, :], OX)
-    copy(["of1"], ["gl.v"], T.gl[:, 16:20], T.of1[:, 4 * me:4 * me + 4])
+    op("g", g.affine_select, ["xt"], ["x2s"], T.x2s[0:16, :], OX, [[0, P]], A.is_gt, 0.0, 1, 0)
+    look(tab, X, b("ofz"), "ofz", b("gm"), "gm", CH)
     picks("0", OWN, E0)
+    iota("slot.own", b("slot", 0, 128, S0 + ID0 + IDS * me, S0 + ID0 + IDS * me + IDS), [[1, IDS]], Z, 0)
+    iota("sl0", b("sl0"), [[1, (N - 1) * E0]], OWN, 0)
+    iota("sl1", b("sl1"), [[1, (N - 1) * E1]], W1, 0)
+    copy(["of1"], ["gl.v"], T.gl[:, 16:20], T.of1[:, 4 * me:4 * me + 4])
     copy(["old1", "ofz"], X, tab.indirect(b("ofz")), b("old1"))
 
     tt(X + ["gl", "gl.v", "a0", "a0v"], ["ei"], b("ei"), tab.indirect(b("gl")), b("a0"), A.not_equal)
@@ -378,7 +388,7 @@ def rank_program(g, core, T, topo):
     def slots(keys, c0, c1):
         k = "ids%d" % c0
         tsc(keys, [k], b("ids", 0, 128, c0, c1), T.idw[:, c0:c1], 1.0 / 4096, A.mult, S0 - 0.375, A.add)
-        copy([k], ["idu%d" % c0], T.idu[:, c0:c1], b("ids", 0, 128, c0, c1))
+        op("v", g.vector.tensor_copy, [k], ["idu%d" % t for t in range(c0, c1, 16)], T.idu[:, c0:c1], b("ids", 0, 128, c0, c1))
 
     def stand(c0, c1):
         gk, w, n = "gs%d" % c0, slice(16 * c0, 16 * c1), 16 * (c1 - c0)
@@ -407,24 +417,23 @@ def rank_program(g, core, T, topo):
             copy(["acc%d" % i], ["ys%d" % i], T.ys[:, w], T.acc[:, 512 * i:512 * i + P], es[o])
             dma("y", "dy", 16 * R * O, ["ys%d" % i], ["y%d" % i], T.y[:, w], T.ys[:, w])
 
-    fill_slots("0")
-    slots(["idw0"], 0, 16)
-    stand(0, 16)
-    pack(1)
+    diag("ofw", "dd")
+    pack(0)
     picks("1", W1, E1)
+    copy(["old2", "ofw"], X, tab.indirect(b("ofw")), b("old2"))
+    dma("y", "di3", 16, ["xt"], ["idw3"], T.idw[:, 48:64], T.xt[0:8, OB:OB + P])
+    slots(["idw0", "idw1", "idw2"], 0, 48)
+    fill_slots("0")
+    stand(0, 16)
     place(0)
     products(0)
     out(0, "aa")
-    tb("gm", "old2", "mask", A.mult)
-    diag("ofw", "dd")
-    copy(["old2", "ofw"], X, tab.indirect(b("ofw")), b("old2"))
-    dma("y", "di3", 16, ["xt"], ["idw3"], T.idw[:, 48:64], T.xt[0:8, OB:OB + P])
-    slots(["idw1", "idw2"], 16, 48)
     fill_slots("1")
     stand(16, 48)
     place(1)
-    place(2)
     products(1)
+    place(2)
+    pack(1)
     products(2)
     out(1, "aa")
     slots(["idw3"], 48, 64)

@@ -3,11 +3,10 @@ from concourse.mybir import dt, AluOpType as A, ActivationFunctionType as F
 
 N, P, V, R, O = 8, 256, 64, 4, 2
 CH = N * V
-D0 = 2 * CH
-RS = P + 2 * V
-XW = D0 + N * P
+NP = N * P
+AD = 8
 IDS = P + V
-ID0 = 8
+NO = NP + CH + 8
 S0 = 512
 Z = 32
 E0, E1 = 16, 48
@@ -18,8 +17,11 @@ IT = P + V
 K0, K1 = 64, 200
 C0, C1 = 7, 21
 W = {"0": 1, "1": 3}
+CC = {"0": C0, "1": C1}
+KK = {"0": K0, "1": K1}
 
-SCRATCH = {"lists": ("dram", [8, 128, 4], "float32"), "acc": ("psum", [128, 4096], "float32")}
+SCRATCH = {"lists": ("dram", [8, 128, 4], "float32"), "hbd": ("dram", [128, 4], "int32"), "idd": ("dram", [64, 4], "float32"),
+           "acc": ("psum", [128, 4096], "float32")}
 POOL = {}
 
 
@@ -37,21 +39,21 @@ def _pool(buf, dtype, **cols):
     SCRATCH[buf] = ("sbuf", [128, a], dtype)
 
 
-_sb("int32", src=4, pi=1, rowb=RS, hb=RS, dd=32, de=32, gli=20)
-_sb("float32", sv=4, e16=4, jm=16, gm=CH, scn=CH, old1=CH, old2=CH, f1f=32,
-    vf=4 * CH, xt=XW, a0=IT, x1s=P, x2s=P, x3s=P, ei=IT, gg=IT, pf=IT, qq=IT, tq=IT, ts=IT, val=160, val0=32, pl0=208,
-    pl1=560, la0=C0, lb0=C0, la1=C1, lb1=C1, slot=S0 + ID0 + N * IDS + 24, sl0=(N - 1) * E0, sl1=(N - 1) * E1,
-    idw=64, gs=4 * P, gsc=4 * P, ys=2048, dcol=1, b16=1, b48=1)
+_sb("int32", src=4, shh=4, pi=1, row1=V, hb1=V, row0=IT, dd=32, gli=20)
+_sb("float32", sv=4, k4=4, idc=4, idf=4, jm=16, gm0=CH, gm1=CH, gm2=CH, tr=CH, f1f=32, v1=CH, v2=CH, xt=3 * NP, yt=NP, a0=IT,
+    x1s=P, x2s=P, x3s=P, ei=IT, gg=IT, pf=IT, qq=IT, tq=IT, ts=IT, val=160, val0=32, vp0=32, vm0=32, pl0=208,
+    pl1=560, la0=C0, lb0=C0, ma0=C0, mb0=C0, la1=C1, lb1=C1, ma1=C1, mb1=C1, slot=S0 + NO + 8, sl0=(N - 1) * E0,
+    sl1=(N - 1) * E1, idw=64, gs=4 * P, gsc=4 * P, ys=2048, dcol=1, b16=1, b48=1)
 _sb("uint16", of1=32, ofq=32, ofz=32, ofw=32, gl=20, ofp=10, ofp0=2, pk0u=C0, pk1u=C1, mt0u=C0, mt1u=C1, meta0=C0, meta1=C1, idu=64,
     so=64)
-_sb("bfloat16", cv=4 * OWN, wt=4096, ones=IT, k32=IT, md=RS, mask=CH, keep=CH)
+_sb("bfloat16", cv=4 * OWN, wt=4096, ones=IT, k32=IT, md=IT, md1=V, mask=CH, keep=CH)
 _sb("float8_e4m3fn_x4", wq=1024, qo=OWN, sn0=112, sn1=336, fw=WW, pk0=P, pk1=P, pk2=P, pk3=P)
 _sb("uint8", wqs=1024, qos=OWN, sn0s=112, sn1s=336, fws=WW, ps0=P, ps1=P, ps2=P, ps3=P)
-_pool("tf", "float32", sxx=4, sxh=4, k2=4, k2a=4, sa=4, sb=4, sc=4, s1=4, s2=4, s3=4, sm=4, c64=1, cm=1, c16=1, ck=1, pmf=1,
-      ne2=V, mt0=C0, mt1=C1)
-_pool("ti", "int32", sy=4, shh=4, pa3=1, pa2=1, pm=1, lo=10, hi=10, l2=10, sm2=10, mx2=10, wi=32, wn=32, wm=32, ids=64)
-SEMAPHORES = ["vv", "aa", "pp", "gq", "lsent", "aL", "aM0", "aC0", "aS0", "aM1", "aC1", "aS1", "dsrc", "drow", "dcv", "dw0", "dw1",
-              "dfw", "down", "dfan", "df1", "dvf", "dpl0", "dpl1", "di0", "di1", "di2", "di3", "dy"]
+_pool("tf", "float32", sa=4, sb=4, sc=4, s1=4, s2=4, em=4, pmf=1, px0=C0, px1=C1, mt0=C0, mt1=C1)
+_pool("ti", "int32", sy=4, pm=1, lo=10, hi=10, l2=10, sm2=10, mx2=10)
+SEMAPHORES = ["vv", "aa", "pp", "gq", "lsent", "aL", "aM0", "aC0", "aS0", "aM1", "aC1", "aS1", "dsrc", "drow", "dhb", "dhd", "did",
+              "demp", "dcv", "dw0", "dw1", "dfw", "down", "dfan", "df1", "dv1", "dpl0", "dpl1", "dpm0", "dpm1", "di0", "di1", "di2",
+              "di3", "dy"]
 
 
 def rank_program(g, core, T, topo):
@@ -60,8 +62,8 @@ def rank_program(g, core, T, topo):
         return
     cores = T.cores
     others = [d for d in range(N) if d != me]
-    OB = D0 + P * me
-    SM = S0 + ID0 + IDS * me - Z
+    OB = P * me
+    VB = NP + V * me
     q = {"v": g.vector, "a": g.scalar, "p": g.tensor, "g": g, "y": g.sync}
     csem = {"v": "vv", "a": "aa", "p": "pp", "g": "gq"}
     cnt = {"v": 0, "a": 0, "p": 0, "g": 0}
@@ -109,11 +111,13 @@ def rank_program(g, core, T, topo):
         for k in reads:
             rd.setdefault(k, []).append(tok)
 
-    def copy(reads, writes, out, in_, e="v"):
+    def copy(reads, writes, out, in_, e="v", plus=None):
         if e == "v":
             op("v", g.vector.tensor_copy, reads, writes, out, in_)
-        else:
+        elif plus is None:
             op("a", g.scalar.activation, reads, writes, out, in_, F.Copy)
+        else:
+            op("a", g.scalar.activation, reads, writes, out, in_, F.Identity, bias=float(plus))
 
     def tsc(reads, writes, out, in0, s1, op0, s2=None, op1=None):
         if op1 is None:
@@ -178,97 +182,86 @@ def rank_program(g, core, T, topo):
         w = slice(512 * h, 512 * h + 512)
         op("v", g.vector.quantize_mx, ["wt%d" % h], ["wq%d" % h], T.wq[:, w], T.wqs[:, w], T.wt[:, 2048 * h:2048 * h + 2048])
 
-    dma("y", "dsrc", 128, [], ["src"], T.src[0:64, :], T.alt[:, :])
-    dma("y", "dsrc", 128, [], ["src"], T.src[64:128, 0:1], T.f1[:, :])
-    dma("y", "dsrc", 128, [], ["src"], T.src[64:128, 1:2], T.f2[:, :])
+    dma("y", "dsrc", 224, [], ["src"], T.src[0:64, :], T.alt[:, :])
     for c in range(4):
-        dma("a", "dsrc", 128, [], ["src"], T.src[64 + c // 2:96:2, 2 + c % 2:3 + c % 2], T.f1[4 * c:4 * c + 4, :])
-    dma("y", "dsrc", 128, [], ["src"], T.src[96:128, 2:4], T.f1[:, :])
+        dma("a", "dsrc", 224, [], ["src"], T.src[64:80, c:c + 1], T.f1[4 * c:4 * c + 4, :])
+    dma("y", "dsrc", 224, [], ["src"], T.src[96:112, :], T.f2[:, :])
+    for c in range(4):
+        x = c + 1 - 2 * (c % 2)
+        dma("a", "dsrc", 224, [], ["src"], T.src[80:96, c:c + 1], T.f1[4 * x:4 * x + 4, :])
+        dma("y", "dsrc", 224, [], ["src"], T.src[112 + 4 * c:116 + 4 * c, :], T.f2[4 * x:4 * x + 4, :])
     for p in range(N):
-        for lo, t in ((0, T.alt), (P, T.f2), (IT, T.f1)):
-            dma("ya"[p % 2], "drow", 16 * 3 * N, [], ["rowb"], T.rowb[p:p + 1, lo:lo + (P if lo == 0 else V)], t[:, :])
+        dma("ya"[p % 2], "drow", 16 * N, [], ["row1"], T.row1[p:p + 1, :], T.f1[:, :])
     dma("y", "dcv", 32, [], ["cv.c"], T.cv[:, 4 * Z:4 * (Z + P)], T.c[:, :])
     dma("y", "dcv", 32, [], ["cv.c"], T.cv[:, 4 * (Z + P):4 * OWN], T.v[:, :])
-
-    iota("pi", b("pi"), [[1, 1]], 0, 1, False)
-    iota("e16", b("e16"), [[16, 4]], 0, 0)
-    iota("dd", b("dd"), [[16, 32]], 0, 1, False)
-    iota("jm", b("jm"), [[1, 16]], 0, 0)
-    iota("f1o", b("f1f"), [[16, 32]], 0, 1)
-    iota("dcol", b("dcol"), [[1, 1]], 0, 1)
-    iota("dcol", b("dcol", 0, me + 1), [[1, 1]], 99, 0)
-    if me:
-        iota("dcol", b("dcol", 0, me), [[1, 1]], 0, 1)
 
     def begin(nm, e, k):
         iota(nm, b(nm), [[1, 1]], 16 * k - 1 - e, e)
         iota(nm, b(nm, 0, me + 1), [[1, 1]], 16 * k - 1, e)
 
-    begin("b16", E0, K0)
-    fill("md", T.md[0:32, :], 0.0)
-    own0 = float(ID0 + IDS * me)
-    sb("pa3", "pi", 3, A.bitwise_and)
-    sb("pa2", "pi", 2, A.arith_shift_right)
-    fill("sxx", b("sxx"), 16.0)
-    fill("sxh", b("sxh"), 240.0)
-    fill("k2", b("k2", 64), float(D0))
-    sb("c64", "pa3", 64.0, A.mult)
-    sb("c16", "pa3", 16.0, A.mult)
-    fill("sxx", b("sxx", 64, 128, 0, 1), 16.0 + 4096.0)
-    fill("sxh", b("sxh", 64, 128, 0, 1), 240.0 + 4096.0 * (IDS - P))
-    fill("k2", b("k2", 64, 128, 0, 1), D0 + 4096.0 * ID0)
-    tb("cm", "c64", "pa2", A.add)
-    tb("ck", "c16", "pa2", A.add)
-    tsc(["e16", "cm"], ["k2a"], b("k2a", 0, 64), b("e16", 0, 64), b("cm", 0, 64), A.add, 4096.0, A.mult)
-    tsc(["ck"], ["k2"], b("k2", 64, 128, 1, 2), b("ck", 64), 4096.0, A.mult, D0 + 4096.0 * (own0 + P - 16), A.add)
-    tsc(["k2a"], ["k2"], b("k2", 0, 64), b("k2a", 0, 64), D0 + 4096.0 * own0, A.add)
-
-    sb("sy", "src", 4, A.arith_shift_right)
-    sb("shh", "src", 8, A.arith_shift_right)
-    tb("sa", "src", "sxx", A.mult)
-    sb("sm", "src", 0.0, A.is_ge)
-    sb("sb", "sy", -255.0, A.mult)
-    tb("sc", "shh", "sxh", A.mult)
-    tb("s1", "sa", "k2", A.add)
-    tb("s2", "sb", "sc", A.add)
-    tb("s3", "s1", "s2", A.add)
-    tb("sv", "s3", "sm", A.mult)
-    need("g", wr["sv"])
-    spread("aL", lambda d: (b("sv"), T.lists[me]))
-    dma("y", "down", 16, ["sv"], ["lown"], T.lists[me], b("sv"))
-    load_w("y", 0)
-
-    fill("xt.z", T.xt[:, 0:CH], 0.0)
-    copy(["xt.z"], ["xt.d"], T.xt[:, CH:2 * CH], T.xt[:, 0:CH], "a")
-    copy(["xt.z"], ["xt.d"], T.xt[:, D0:D0 + 128], T.xt[:, 0:128], "a")
-    for k in range(2):
-        copy(["xt.z"], ["vf"], T.vf[:, k:4 * CH:4], T.xt[:, 0:CH], "a")
-
+    iota("k4", b("k4"), [[1, 4]], NP + OB, 4)
+    iota("dd", b("dd"), [[16, 32]], 0, 1, False)
+    iota("yt", T.yt[:, 0:256], [[1, 256]], 0, 0)
+    iota("idc", b("idc"), [[1, 4]], OB, 4)
     fill("pl0", b("pl0", 0, 32, K0, K0 + 16 * C0), 0.0)
-    for r1, k in ((128, 4), (16, 0)):
-        iota("val0", b("val0", 0, r1), [[8, 2], [1, 4], [16, 4]], SM + Z + P + k, 0)
     iota("pl0", b("pl0", 0, 16, K0, K0 + 16 * C0), [[1, 16], [0, N - 1]], E0 * me, 0)
-    iota("gli", b("gli"), [[16, 20]], 0, 1, False)
-    iota("gli", b("gli", 0, 16), [[16, 20]], OB, 1, False)
-    iota("de", b("de"), [[16, 32]], CH, 1, False)
-    begin("b48", E1, K1)
-    iota("pl1", b("pl1", 0, 32, K1, K1 + 16 * C1), [[0, 16 * C1]], 0, 0)
-    iota("pl1", b("pl1", 0, 16, K1, K1 + 16 * C1), [[1, 16], [0, N - 1], [16, 3]], E1 * me, 0)
-    for r1, k in ((128, 4), (16, 0)):
-        iota("val.c", b("val", 0, r1, 0, 128), [[2, 8], [16, 16]], SM + Z + k // 4, 0)
-        iota("val.v", b("val", 0, r1, 128, 160), [[8, 2], [1, 4], [16, 4]], SM + Z + P + k, 0)
-
+    iota("dcol", b("dcol"), [[1, 1]], 0, 1)
+    iota("dcol", b("dcol", 0, me + 1), [[1, 1]], 99, 0)
+    if me:
+        iota("dcol", b("dcol", 0, me), [[1, 1]], 0, 1)
+    begin("b16", E0, K0)
+    iota("vp0", b("vp0"), [[8, 2], [1, 4], [16, 4]], Z + P, 0)
+    iota("vm0", b("vm0"), [[32, 2], [1, 16]], S0 + VB, 0)
     fill("ones", b("ones"), 1.0)
     fill("k32", b("k32"), 1.0)
     fill("k32", T.k32[:, 0:IT:32], 0.0)
-    tsc(["rowb"], ["hb"], T.hb[0:N, :], T.rowb[0:N, :], 8, A.arith_shift_right)
-    tsc(["hb", "dcol"], ["md"], T.md[0:N, :], T.hb[0:N, :], b("dcol", 0, N), A.is_equal)
+    fill("md", T.md[0:32, :], 0.0)
+    fill("md1", T.md1[0:32, :], 0.0)
+    fill("val0", b("val0"), 0.0)
+    fill("slot.z", T.slot[:, S0 + NO:S0 + NO + 8], 0.0)
+    fill("cv.z", T.cv[:, 0:4 * Z], 0.0)
+    fill("keep", T.keep[:, 0:16], 1.0)
+    fill("keep", T.keep[:, 0:1], 0.0)
+    for nm in ("of1", "ofq", "ofz", "ofw"):
+        copy(["dd"], [nm], b(nm), b("dd"))
     copy(["dd"], ["ofp0"], b("ofp0"), T.dd[:, 0:2])
     copy(["dd"], ["ofp"], b("ofp"), T.dd[:, 0:10])
-    sb("pm", "pi", 15, A.bitwise_and)
-    fill("cv.z", T.cv[:, 0:4 * Z], 0.0)
-    copy(["pm"], ["pmf"], b("pmf"), b("pm"))
-    op("v", g.vector.quantize_mx, ["cv.z", "cv.c"], ["qo.own"], T.qo[:, 0:OWN], T.qos[:, 0:OWN], T.cv[:, :])
+
+    sb("sy", "src", 4, A.arith_shift_right)
+    sb("shh", "src", 8, A.arith_shift_right, 4095, A.bitwise_and)
+    sb("sa", "src", 16.0, A.mult)
+    sb("sb", "sy", -255.0, A.mult)
+    sb("sc", "shh", 240.0, A.mult)
+    tb("s1", "sa", "sb", A.add)
+    tb("s2", "s1", "sc", A.add)
+    tb("sv", "s2", "k4", A.min)
+    need("g", wr["sv"])
+    spread("aL", lambda d: (b("sv"), T.lists[me]))
+    tsc(["src"], ["em"], b("em"), b("src"), 0.0, A.is_lt, float(NO), A.mult)
+    tb("idf", "em", "idc", A.max)
+    dma("y", "dhd", 16, ["shh"], ["hbd"], T.hbd[:, :], b("shh"))
+    dma("y", "down", 16, ["sv"], ["lown"], T.lists[me], b("sv"))
+    dma("y", "did", 16, ["idf"], ["idd"], T.idd[:, :], T.idf[0:64, :])
+    for p in range(N):
+        dma("y", "dhb", 32 * N, ["hbd"], ["row0"], T.row0[p:p + 1, 0:P], T.hbd[0:64, :])
+        dma("y", "dhb", 32 * N, ["hbd"], ["row0"], T.row0[p:p + 1, P:IT], T.hbd[96:112, :])
+
+    for n in (256, 512, 1024):
+        copy(["yt"], ["yt"], T.yt[:, n:2 * n], T.yt[:, 0:n], "a", n)
+    copy(["yt"], ["xt"], T.xt[:, 0:NP], T.yt[:, :], "a")
+    wr["xf"] = wr["xt"]
+    copy(["yt"], ["v1"], b("v1"), T.yt[:, 0:CH], "a", NP)
+
+    iota("jm", b("jm"), [[1, 16]], 0, 0)
+    iota("pi", b("pi"), [[1, 1]], 0, 1, False)
+    iota("gli", b("gli"), [[16, 20]], 0, 1, False)
+    iota("gli", b("gli", 0, 16), [[16, 20]], OB, 1, False)
+    begin("b48", E1, K1)
+    for k, rm, rw in ((1, 128, 24), (0, 16, 8)):
+        iota("val.c", b("val", 0, rm, 0, 128), [[32, 8], [1, 16]], S0 + OB + 16 * k, 0)
+        iota("val.c", b("val", 0, rw, 0, 128), [[2, 8], [16, 16]], Z + k, 0)
+        iota("val.v", b("val", 0, rm, 128, 160), [[32, 2], [1, 16]], S0 + VB + 16 * k, 0)
+        iota("val.v", b("val", 0, rw, 128, 160), [[8, 2], [1, 4], [16, 4]], Z + P + 4 * k, 0)
 
     def compact(n, marks, key, base, width, of, val, vkeys, pl):
         k = n // 32
@@ -288,52 +281,77 @@ def rank_program(g, core, T, topo):
         copy(["mx2"], [of], s(of), s("mx2"))
         copy([of] + vkeys, [pl], T[pl][:, :].indirect(T[of][:, 0:k]), T[val][:, :])
 
-    compact(V, T.md[0:32, IT:RS], "md", "b16", C0, "ofp0", "val0", ["val0"], "pl0")
-    tt(["hb"], ["ne2"], b("ne2", 0, N), T.hb[0:N, P:IT], T.hb[0:N, IT:RS], A.not_equal)
-    tt(["ne2", "md"], ["md"], T.md[0:N, P:IT], T.md[0:N, P:IT], b("ne2", 0, N), A.mult)
-    fill("keep", b("keep"), 1.0)
-    fill("keep", T.keep[:, 0:CH:16], 0.0)
-    tsc(["jm", "pmf"], ["mask"], T.mask[:, 0:16], b("jm"), b("pmf"), A.is_equal)
-    n = 16
-    while n < CH:
-        copy(["mask"], ["mask"], T.mask[:, n:2 * n], T.mask[:, 0:n])
-        n *= 2
-    fill("slot.z", T.slot[:, S0:S0 + ID0], 0.0)
+    def wrap(k):
+        c, a = CC[k], KK[k]
+        both = [("dpm", 8, ("ma", "mb")), ("dpl", 0, ("la", "lb"))]
+        for sem, r, nms in both if k == "1" else both[::-1]:
+            for i, nm in enumerate(nms):
+                dma("y", sem + k, 32, ["pl" + k], [nm + k], b(nm + k), T["pl" + k][16 * i + r:16 * i + r + 8, a:a + 16 * c])
+
+    for r1, nm, plus in ((32, "vm0", 16), (24, "vp0", 4), (16, "vm0", 0), (8, "vp0", 0)):
+        tsc([nm], ["val0"], b("val0", 0, r1), b(nm, 0, r1), float(plus), A.add)
+    fill("pl0", b("pl0", 0, 8, K0, K0 + 16 * C0), 0.0)
+    tsc(["row1"], ["hb1"], T.hb1[0:N, :], T.row1[0:N, :], 8, A.arith_shift_right)
+    tsc(["hb1", "dcol"], ["md1"], T.md1[0:N, :], T.hb1[0:N, :], b("dcol", 0, N), A.is_equal)
+    compact(V, T.md1[0:32, :], "md1", "b16", C0, "ofp0", "val0", ["val0"], "pl0")
+    wrap("0")
+    for p in range(N):
+        dma("y", "demp", 16 * N, ["idd", "xf"], ["xo"], T.xt[p:p + 1, OB:OB + P], T.idd[:, :])
+    op("v", g.vector.quantize_mx, ["cv.z", "cv.c"], ["qo.own"], T.qo[:, 0:OWN], T.qos[:, 0:OWN], T.cv[:, :])
     copy(["gli"], ["gl"], T.gl[:, 0:16], T.gli[:, 0:16])
+    sb("pm", "pi", 15, A.bitwise_and)
+    copy(["pm"], ["pmf"], b("pmf"), b("pm"))
+    tsc(["jm", "pmf"], ["mask"], T.mask[:, 0:16], b("jm"), b("pmf"), A.is_equal)
+    tsc(["row0", "dcol"], ["md"], T.md[0:N, :], T.row0[0:N, :], b("dcol", 0, N), A.is_equal)
 
     arrive("aL", "lfar")
-    for e, half in (("y", 0), ("a", 1)):
-        for p in range(8 * half, 8 * half + 8):
-            dma(e, "dfan", 256, ["lfar", "lown"], ["xt", "xt.d", "xt.z"], T.xt[p:p + 1, D0:XW], T.lists[:, 0:64, :])
-        for h in range(4 * half, 4 * half + 4):
-            dma(e, "df1", 128, ["lfar", "lown"], ["f1o"], T.f1f[0:16, 4 * h:4 * h + 4], T.lists[h, 64:96, 2:4])
-        for p in range(8 * half, 8 * half + 8):
-            dma(e, "dvf", 256, ["lfar", "lown"], ["vf"], T.vf[p:p + 1, :], T.lists[:, 64:128, :])
-    copy(["xt.z"], ["a0"], b("a0"), T.xt[:, 0:IT], "a")
-    for nm, r0 in (("la0", 0), ("lb0", 16)):
-        dma("y", "dpl0", 32, ["pl0"], [nm], b(nm), T.pl0[r0:r0 + 8, K0:K0 + 16 * C0])
+    for r in range(N):
+        dma("y", "df1", 128, ["lfar", "lown"], ["f1f"], T.f1f[0:32, 4 * r:4 * r + 4], T.lists[r, 64:96, :])
+    for h in range(2):
+        p = 16 * h + AD
+        dma("a", "dfan", 32, ["lfar", "lown"], ["xt"], T.xt[p:p + 1, 0:NP], T.lists[:, 0:64, :])
+    for h in range(2):
+        p = 16 * h + AD
+        dma("a", "dv1", 32, ["lfar", "lown"], ["v1"], T.v1[p:p + 1, :], T.lists[:, 96 + 16 * h:112 + 16 * h, :])
+    load_w("y", 0)
     load_w("y", 1)
     dma("y", "dfw", 32, ["qo.own"], ["fw.own"], T.fw[:, 0:OWN].bitcast(dt.uint8), T.qo[:, 0:OWN].bitcast(dt.uint8))
     dma("y", "dfw", 32, ["qo.own"], ["fw.own"], T.fws[:, 0:OWN], T.qos[:, 0:OWN])
+    copy(["yt"], ["x1"], T.xt[:, NP:2 * NP], T.yt[:, :], "a", 2 * NP)
 
     def look(table, keys, of, ok, gm, gk, n):
         tt(keys + [ok, "mask"], [gk], gm, table.indirect(of), T.mask[:, 0:n], A.mult)
 
-    def diag(of, dump):
-        scan(["gm", "keep"], ["scn"], b("scn"), b("keep"), b("gm"), 0.0)
-        copy(["scn"], ["wi"], b("wi"), T.scn[:, 15:CH:16])
-        sb("wn", "wi", 4095, A.bitwise_and)
-        tb("wm", "wn", dump, A.max)
-        copy(["wm"], [of], b(of), b("wm"))
+    X = ["xt", "x1", "x2"]
 
-    def picks(k, first, e):
-        la, lb, pku, dst, dss, meta, mt = [x + k for x in ("la", "lb", "pk", "sn", "sn", "meta", "mt")]
-        pku, dss, mtu, w = pku + "u", dss + "s", mt + "u", W[k]
-        tb(mt, la, lb, A.max)
-        tsc([mt], [pku], b(pku), b(mt), -float(SM), A.add, 0.0, A.max)
-        copy([mt], [mtu], b(mtu), b(mt))
+    def step(t, of, gm):
+        copy(X[0:t + 1] + ["xo", of], [gm], b(gm), T.xt[:, 0:NP * (t + 1)].indirect(b(of)))
+
+    def turn(gm, of):
+        op("v", g.vector.transpose, [gm], ["tr"], T.tr[0:32, :], T[gm][0:32, :])
+        copy(["tr"], [of], b(of, 0, 32), T.tr[0:32, AD:CH:16])
+
+    def put(t, of, val):
+        copy([of, val], X[0:t + 1], T.xt[:, 0:NP * (t + 1)].indirect(b(of)), b(val))
+
+    def picks(k):
+        la, lb, ma, mb, pku, dst, px, mt = [x + k for x in ("la", "lb", "ma", "mb", "pk", "sn", "px", "mt")]
+        pku, dss, mtu = pku + "u", dst + "s", mt + "u"
+
+        def slots_of():
+            tb(mt, ma, mb, A.max)
+            copy([mt], [mtu], b(mtu), b(mt))
+        if k == "1":
+            slots_of()
+        tb(px, la, lb, A.max)
+        copy([px], [pku], b(pku), b(px))
         copy(["qo.own", pku], [dst], b(dst).bitcast(dt.uint32), b("qo").bitcast(dt.uint32).indirect(b(pku)))
         copy(["qo.own", pku], [dss], b(dss), b("qos").indirect(b(pku)), "a")
+        if k == "0":
+            slots_of()
+
+    def send(k, first, e):
+        mtu, meta, dst, dss, w = "mt" + k + "u", "meta" + k, "sn" + k, "sn" + k + "s", W[k]
         need("g", wr[mtu])
         spread("aM" + k, lambda d: (T[mtu][:, w * at(d, me):w * at(d, me) + w], T[meta][:, w * at(me, d):w * at(me, d) + w]))
         need("g", wr[dst])
@@ -346,49 +364,55 @@ def rank_program(g, core, T, topo):
         arrive("aC" + k, "fw" + k)
         arrive("aS" + k, "fws" + k)
 
-    X = ["xt", "xt.d", "xt.z"]
-    tab = T.xt[:, :]
-    OX = T.xt[0:16, OB:OB + P]
-    v2, v1 = T.vf[:, 0:4 * CH:4], T.vf[:, 1:4 * CH:4]
-    copy(["xt"], ["a0"], T.a0[0:16, 0:P], OX, "a")
-    copy(["vf"], ["a0v"], T.a0[0:16, P:IT], T.vf[0:16, 4 * V * me + 1:4 * V * me + 4 * V:4], "a")
-    copy(["f1o"], ["of1"], b("of1"), b("f1f"))
-    look(tab, X, b("of1"), "of1", b("gm"), "gm", CH)
-    diag("ofq", "dd")
-    copy(["vf", "of1"], X, tab.indirect(b("of1")), v1)
-    copy(["xt"], ["x1s"], T.x1s[0:16, :], OX, "a")
-    copy(X + ["ofq"], ["old1"], b("old1"), tab.indirect(b("ofq")), "a")
-    look(tab, X, b("ofq"), "ofq", b("gm"), "gm", CH)
-    diag("ofz", "de")
-    copy(["vf", "ofq"], X, tab.indirect(b("ofq")), v2)
-    copy(X + ["ofz"], ["old2"], b("old2"), tab.indirect(b("ofz")), "a")
-    op("g", g.affine_select, ["xt"], ["x2s"], T.x2s[0:16, :], OX, [[0, P]], A.is_gt, 0.0, 1, 0)
-    look(tab, X, b("ofz"), "ofz", b("gm"), "gm", CH)
-    picks("0", OWN, E0)
-    iota("slot.own", b("slot", 0, 128, S0 + ID0 + IDS * me, S0 + ID0 + IDS * me + IDS), [[1, IDS]], Z, 0)
+    picks("0")
+    copy(["f1f"], ["of1"], b("of1", 0, 32), b("f1f", 0, 32))
+    copy(["yt", "of1"], ["v2"], b("v2"), b("yt").indirect(b("of1")), "a")
+    step(0, "of1", "gm0")
+    need("g", wr["of1"])
+    send("0", OWN, E0)
+    iota("a0", b("a0", 0, 128, 0, P), [[1, P]], OB, 0)
+    iota("a0.v", b("a0", 0, 128, P, IT), [[1, V]], VB, 0)
+    iota("pl1", b("pl1", 0, 32, K1, K1 + 16 * C1), [[0, 16 * C1]], 0, 0)
+    iota("pl1", b("pl1", 0, 16, K1, K1 + 16 * C1), [[1, 16], [0, N - 1], [16, 3]], E1 * me, 0)
+    iota("pl1", b("pl1", 0, 8, K1, K1 + 16 * C1), [[0, 16 * C1]], 0, 0)
+    iota("slot.own", b("slot", 0, 128, S0 + OB, S0 + OB + P), [[1, 16], [16, 16]], Z, 0)
+    iota("slot.own", b("slot", 0, 128, S0 + VB, S0 + VB + V), [[1, 16], [16, 4]], Z + P, 0)
     iota("sl0", b("sl0"), [[1, (N - 1) * E0]], OWN, 0)
     iota("sl1", b("sl1"), [[1, (N - 1) * E1]], W1, 0)
-    copy(["of1"], ["gl.v"], T.gl[:, 16:20], T.of1[:, 4 * me:4 * me + 4])
-    copy(["old1", "ofz"], X, tab.indirect(b("ofz")), b("old1"))
 
-    tt(X + ["gl", "gl.v", "a0", "a0v"], ["ei"], b("ei"), tab.indirect(b("gl")), b("a0"), A.not_equal)
-    tt(["ei", "md"], ["gg"], T.gg[0:32, :], T.ei[0:32, :], T.md[0:32, 0:IT], A.mult)
+    OX = T.xt[0:16, OB:OB + P]
+    put(0, "of1", "v1")
+    copy(["xt"], ["x1s"], T.x1s[0:16, :], OX, "a")
+    copy(["yt"], ["x2"], T.xt[:, 2 * NP:3 * NP], T.yt[:, :], "a", 2 * NP)
+    turn("gm0", "ofq")
+    step(1, "ofq", "gm1")
+    put(1, "ofq", "v2")
+    copy(["xt"], ["x2s"], T.x2s[0:16, :], OX, "a")
+    turn("gm1", "ofz")
+    step(2, "ofz", "gm2")
+    copy(["of1"], ["gl.v"], T.gl[:, 16:20], T.of1[:, 4 * me:4 * me + 4])
+    put(2, "ofz", "gm1")
+
+    tt(["xt", "gl", "gl.v", "a0", "a0.v"], ["ei"], b("ei"), T.xt[:, 0:NP].indirect(b("gl")), b("a0"), A.not_equal)
+    tt(["ei", "md"], ["gg"], T.gg[0:32, :], T.ei[0:32, :], T.md[0:32, :], A.mult)
     compact(IT, T.gg[0:32, :], "gg", "b48", C1, "ofp", "val", ["val.c", "val.v"], "pl1")
     for t, nm in enumerate(("x1s", "x2s")):
         dma("y", "di%d" % t, 16, [nm], ["idw%d" % t], T.idw[:, 16 * t:16 * t + 16], T[nm][0:8, :])
-    for nm, r0 in (("la1", 0), ("lb1", 16)):
-        dma("y", "dpl1", 32, ["pl1"], [nm], b(nm), T.pl1[r0:r0 + 8, K1:K1 + 16 * C1])
+    wrap("1")
     copy(["xt"], ["x3s"], T.x3s[0:16, :], OX, "a")
     dma("y", "di2", 16, ["x3s"], ["idw2"], T.idw[:, 32:48], T.x3s[0:8, :])
+    for nm in ("mask", "keep"):
+        n = 16
+        while n < CH:
+            copy([nm], [nm], T[nm][:, n:2 * n], T[nm][:, 0:n], "a")
+            n *= 2
 
     def fill_slots(k):
         copy(["meta" + k, "sl" + k], ["slot", "slot.own", "slot.z"],
              b("slot").indirect(T["meta" + k][:, 0:W[k] * (N - 1)]), b("sl" + k))
 
     def slots(keys, c0, c1):
-        k = "ids%d" % c0
-        tsc(keys, [k], b("ids", 0, 128, c0, c1), T.idw[:, c0:c1], 1.0 / 4096, A.mult, S0 - 0.375, A.add)
-        op("v", g.vector.tensor_copy, [k], ["idu%d" % t for t in range(c0, c1, 16)], T.idu[:, c0:c1], b("ids", 0, 128, c0, c1))
+        tsc(keys, ["idu%d" % t for t in range(c0, c1, 16)], T.idu[:, c0:c1], T.idw[:, c0:c1], float(S0), A.add)
 
     def stand(c0, c1):
         gk, w, n = "gs%d" % c0, slice(16 * c0, 16 * c1), 16 * (c1 - c0)
@@ -417,18 +441,20 @@ def rank_program(g, core, T, topo):
             copy(["acc%d" % i], ["ys%d" % i], T.ys[:, w], T.acc[:, 512 * i:512 * i + P], es[o])
             dma("y", "dy", 16 * R * O, ["ys%d" % i], ["y%d" % i], T.y[:, w], T.ys[:, w])
 
-    diag("ofw", "dd")
-    pack(0)
-    picks("1", W1, E1)
-    copy(["old2", "ofw"], X, tab.indirect(b("ofw")), b("old2"))
+    turn("gm2", "ofw")
+    put(2, "ofw", "gm2")
+    picks("1")
+    send("1", W1, E1)
     dma("y", "di3", 16, ["xt"], ["idw3"], T.idw[:, 48:64], T.xt[0:8, OB:OB + P])
     slots(["idw0", "idw1", "idw2"], 0, 48)
     fill_slots("0")
     stand(0, 16)
     place(0)
+    pack(0)
     products(0)
     out(0, "aa")
     fill_slots("1")
+    slots(["idw3"], 48, 64)
     stand(16, 48)
     place(1)
     products(1)
@@ -436,7 +462,6 @@ def rank_program(g, core, T, topo):
     pack(1)
     products(2)
     out(1, "aa")
-    slots(["idw3"], 48, 64)
     stand(48, 64)
     place(3)
     products(3)

from concourse.bass import DstId, RemoteDMATransfer
from concourse.mybir import dt, AluOpType as A, ActivationFunctionType as F

N, P, V, R, O = 8, 256, 64, 4, 2
CH = N * V
NP = N * P
AD = 8
IDS = P + V
NO = NP + CH + 8
S0 = 512
Z = 32
E0, E1 = 16, 48
OWN = Z + IDS
W1 = OWN + (N - 1) * E0
WW = W1 + (N - 1) * E1
IT = P + V
K0, K1 = 64, 200
C0, C1 = 7, 21
W = {"0": 1, "1": 3}
CC = {"0": C0, "1": C1}
KK = {"0": K0, "1": K1}

SCRATCH = {"lists": ("dram", [8, 128, 4], "float32"), "hbd": ("dram", [128, 4], "int32"), "idd": ("dram", [64, 4], "float32"),
           "acc": ("psum", [128, 4096], "float32")}
POOL = {}


def _sb(dtype, **cols):
    for k in cols:
        SCRATCH[k] = ("sbuf", [128, cols[k]], dtype)
        POOL[k] = (k, 0, cols[k])


def _pool(buf, dtype, **cols):
    a = 0
    for k in cols:
        POOL[k] = (buf, a, cols[k])
        a += cols[k]
    SCRATCH[buf] = ("sbuf", [128, a], dtype)


_sb("int32", src=4, shh=4, pi=1, row1=V, hb1=V, row0=IT, dd=32, gli=20)
_sb("float32", sv=4, k4=4, idc=4, idf=4, jm=16, gm0=CH, gm1=CH, gm2=CH, tr=CH, f1f=32, v1=CH, v2=CH, xt=3 * NP, yt=NP, a0=IT,
    x1s=P, x2s=P, x3s=P, ei=IT, gg=IT, pf=IT, qq=IT, tq=IT, ts=IT, val=160, val0=32, vp0=32, vm0=32, pl0=208,
    pl1=560, la0=C0, lb0=C0, ma0=C0, mb0=C0, la1=C1, lb1=C1, ma1=C1, mb1=C1, slot=S0 + NO + 8, sl0=(N - 1) * E0,
    sl1=(N - 1) * E1, idw=64, gs=4 * P, gsc=4 * P, ys=2048, dcol=1, b16=1, b48=1)
_sb("uint16", of1=32, ofq=32, ofz=32, ofw=32, gl=20, ofp=10, ofp0=2, pk0u=C0, pk1u=C1, mt0u=C0, mt1u=C1, meta0=C0, meta1=C1, idu=64,
    so=64)
_sb("bfloat16", cv=4 * OWN, wt=4096, ones=IT, k32=IT, md=IT, md1=V, mask=CH, keep=CH)
_sb("float8_e4m3fn_x4", wq=1024, qo=OWN, sn0=112, sn1=336, fw=WW, pk0=P, pk1=P, pk2=P, pk3=P)
_sb("uint8", wqs=1024, qos=OWN, sn0s=112, sn1s=336, fws=WW, ps0=P, ps1=P, ps2=P, ps3=P)
_pool("tf", "float32", sa=4, sb=4, sc=4, s1=4, s2=4, em=4, pmf=1, px0=C0, px1=C1, mt0=C0, mt1=C1)
_pool("ti", "int32", sy=4, pm=1, lo=10, hi=10, l2=10, sm2=10, mx2=10)
SEMAPHORES = ["vv", "aa", "pp", "gq", "lsent", "aL", "aM0", "aC0", "aS0", "aM1", "aC1", "aS1", "dsrc", "drow", "dhb", "dhd", "did",
              "demp", "dcv", "dw0", "dw1", "dfw", "down", "dfan", "df1", "dv1", "dpl0", "dpl1", "dpm0", "dpm1", "di0", "di1", "di2",
              "di3", "dy"]


def rank_program(g, core, T, topo):
    me = T.rank_of(core)
    if me is None:
        return
    cores = T.cores
    others = [d for d in range(N) if d != me]
    OB = P * me
    VB = NP + V * me
    q = {"v": g.vector, "a": g.scalar, "p": g.tensor, "g": g, "y": g.sync}
    csem = {"v": "vv", "a": "aa", "p": "pp", "g": "gq"}
    cnt = {"v": 0, "a": 0, "p": 0, "g": 0}
    known, wr, rd, pre = {}, {}, {}, {}

    def b(name, r0=0, r1=128, c0=0, c1=None):
        buf, a, w = POOL[name]
        return T[buf][r0:r1, a + c0:a + (w if c1 is None else c1)]

    def need(e, toks):
        best = {}
        for s, n in toks:
            best[s] = max(best.get(s, 0), n)
        for s in sorted(best):
            if known.get((e, s), 0) < best[s]:
                q[e].wait_ge(T.sem[s], best[s])
                known[(e, s)] = best[s]

    def op(e, fn, reads, writes, *args, **kw):
        toks = []
        for k in reads:
            toks += wr.get(k, [])
        for k in writes:
            toks += wr.get(k, []) + rd.get(k, [])
        need(e, toks)
        cnt[e] += 1
        fn(*args, **kw).then_inc(T.sem[csem[e]], 1)
        tok = (csem[e], cnt[e])
        for k in reads:
            rd.setdefault(k, []).append(tok)
        for k in writes:
            wr[k], rd[k] = [tok], []

    def dma(e, sem, total, reads, writes, out, in_):
        tok, toks = (sem, total), []
        for k in writes:
            if wr.get(k) != [tok]:
                pre[(sem, k)] = wr.get(k, []) + rd.get(k, [])
                wr[k], rd[k] = [tok], []
            toks += pre[(sem, k)]
        for k in reads:
            toks += wr.get(k, [])
        need(e, toks)
        q[e].dma_start(out, in_).then_inc(T.sem[sem], 16)
        for k in reads:
            rd.setdefault(k, []).append(tok)

    def copy(reads, writes, out, in_, e="v", plus=None):
        if e == "v":
            op("v", g.vector.tensor_copy, reads, writes, out, in_)
        elif plus is None:
            op("a", g.scalar.activation, reads, writes, out, in_, F.Copy)
        else:
            op("a", g.scalar.activation, reads, writes, out, in_, F.Identity, bias=float(plus))

    def tsc(reads, writes, out, in0, s1, op0, s2=None, op1=None):
        if op1 is None:
            op("v", g.vector.tensor_scalar, reads, writes, out, in0, s1, None, op0)
        else:
            op("v", g.vector.tensor_scalar, reads, writes, out, in0, s1, s2, op0, op1)

    def tt(reads, writes, out, in0, in1, o):
        op("v", g.vector.tensor_tensor, reads, writes, out, in0, in1, o)

    def tb(out, in0, in1, o):
        tt([in0, in1], [out], b(out), b(in0), b(in1), o)

    def sb(out, in0, s1, op0, s2=None, op1=None):
        tsc([in0], [out], b(out), b(in0), s1, op0, s2, op1)

    def scan(reads, writes, out, d0, d1, initial):
        op("v", g.vector.tensor_tensor_scan, reads, writes, out, d0, d1, initial, A.mult, A.add)

    def fill(key, ap, c):
        op("v", g.vector.memset, [], [key], ap, c)

    def iota(key, out, pattern, base, mult, f=True):
        kw = {"allow_small_or_imprecise_dtypes": True} if f else {}
        op("g", g.iota, [], [key], out, pattern, base, mult, **kw)

    def engines(a, c):
        off = [k for k in cores if k != a and topo.chip(k) != topo.chip(a)]
        on = [k for k in cores if k != a and topo.chip(k) == topo.chip(a)]
        far = topo.engines(a, off[0])
        if c in off:
            n, k = len(far) // len(off), off.index(c)
            return far[n * k:n * k + n]
        near = [x for x in topo.engines(a, c) if x not in far]
        k = on.index(c)
        return near[2 * k:2 * k + 2]

    sent = [0]

    def spread(sem, piece):
        ts = []
        for d in others:
            src, dst = piece(d)
            rid, pid = topo.addr(cores[d])[0:2]
            m = 0
            for x in engines(core, cores[d]):
                m |= 1 << x
                sent[0] += 1
            ts.append(RemoteDMATransfer(dst_ids=[DstId(rid=rid, pnc=pid)], dma_engine_mask=m, remote_sem=T.sem[sem], src=src, dst=dst))
        g.remote_dma_fused(ts, local_sem=T.sem.lsent)

    def arrive(sem, key):
        wr[key] = [(sem, sum(len(engines(cores[s], core)) for s in others))]

    def at(s, d):
        return s if s < d else s - 1

    def load_w(e, h):
        dma(e, "dw%d" % h, 16, [], ["wt%d" % h], T.wt[:, 2048 * h:2048 * h + 2048], T.w[:, 2048 * h:2048 * h + 2048])

    def pack(h):
        w = slice(512 * h, 512 * h + 512)
        op("v", g.vector.quantize_mx, ["wt%d" % h], ["wq%d" % h], T.wq[:, w], T.wqs[:, w], T.wt[:, 2048 * h:2048 * h + 2048])

    dma("y", "dsrc", 224, [], ["src"], T.src[0:64, :], T.alt[:, :])
    for c in range(4):
        dma("a", "dsrc", 224, [], ["src"], T.src[64:80, c:c + 1], T.f1[4 * c:4 * c + 4, :])
    dma("y", "dsrc", 224, [], ["src"], T.src[96:112, :], T.f2[:, :])
    for c in range(4):
        x = c + 1 - 2 * (c % 2)
        dma("a", "dsrc", 224, [], ["src"], T.src[80:96, c:c + 1], T.f1[4 * x:4 * x + 4, :])
        dma("y", "dsrc", 224, [], ["src"], T.src[112 + 4 * c:116 + 4 * c, :], T.f2[4 * x:4 * x + 4, :])
    for p in range(N):
        dma("ya"[p % 2], "drow", 16 * N, [], ["row1"], T.row1[p:p + 1, :], T.f1[:, :])
    dma("y", "dcv", 32, [], ["cv.c"], T.cv[:, 4 * Z:4 * (Z + P)], T.c[:, :])
    dma("y", "dcv", 32, [], ["cv.c"], T.cv[:, 4 * (Z + P):4 * OWN], T.v[:, :])

    def begin(nm, e, k):
        iota(nm, b(nm), [[1, 1]], 16 * k - 1 - e, e)
        iota(nm, b(nm, 0, me + 1), [[1, 1]], 16 * k - 1, e)

    iota("k4", b("k4"), [[1, 4]], NP + OB, 4)
    iota("dd", b("dd"), [[16, 32]], 0, 1, False)
    iota("yt", T.yt[:, 0:256], [[1, 256]], 0, 0)
    iota("idc", b("idc"), [[1, 4]], OB, 4)
    fill("pl0", b("pl0", 0, 32, K0, K0 + 16 * C0), 0.0)
    iota("pl0", b("pl0", 0, 16, K0, K0 + 16 * C0), [[1, 16], [0, N - 1]], E0 * me, 0)
    iota("dcol", b("dcol"), [[1, 1]], 0, 1)
    iota("dcol", b("dcol", 0, me + 1), [[1, 1]], 99, 0)
    if me:
        iota("dcol", b("dcol", 0, me), [[1, 1]], 0, 1)
    begin("b16", E0, K0)
    iota("vp0", b("vp0"), [[8, 2], [1, 4], [16, 4]], Z + P, 0)
    iota("vm0", b("vm0"), [[32, 2], [1, 16]], S0 + VB, 0)
    fill("ones", b("ones"), 1.0)
    fill("k32", b("k32"), 1.0)
    fill("k32", T.k32[:, 0:IT:32], 0.0)
    fill("md", T.md[0:32, :], 0.0)
    fill("md1", T.md1[0:32, :], 0.0)
    fill("val0", b("val0"), 0.0)
    fill("slot.z", T.slot[:, S0 + NO:S0 + NO + 8], 0.0)
    fill("cv.z", T.cv[:, 0:4 * Z], 0.0)
    fill("keep", T.keep[:, 0:16], 1.0)
    fill("keep", T.keep[:, 0:1], 0.0)
    for nm in ("of1", "ofq", "ofz", "ofw"):
        copy(["dd"], [nm], b(nm), b("dd"))
    copy(["dd"], ["ofp0"], b("ofp0"), T.dd[:, 0:2])
    copy(["dd"], ["ofp"], b("ofp"), T.dd[:, 0:10])

    sb("sy", "src", 4, A.arith_shift_right)
    sb("shh", "src", 8, A.arith_shift_right, 4095, A.bitwise_and)
    sb("sa", "src", 16.0, A.mult)
    sb("sb", "sy", -255.0, A.mult)
    sb("sc", "shh", 240.0, A.mult)
    tb("s1", "sa", "sb", A.add)
    tb("s2", "s1", "sc", A.add)
    tb("sv", "s2", "k4", A.min)
    need("g", wr["sv"])
    spread("aL", lambda d: (b("sv"), T.lists[me]))
    tsc(["src"], ["em"], b("em"), b("src"), 0.0, A.is_lt, float(NO), A.mult)
    tb("idf", "em", "idc", A.max)
    dma("y", "dhd", 16, ["shh"], ["hbd"], T.hbd[:, :], b("shh"))
    dma("y", "down", 16, ["sv"], ["lown"], T.lists[me], b("sv"))
    dma("y", "did", 16, ["idf"], ["idd"], T.idd[:, :], T.idf[0:64, :])
    for p in range(N):
        dma("y", "dhb", 32 * N, ["hbd"], ["row0"], T.row0[p:p + 1, 0:P], T.hbd[0:64, :])
        dma("y", "dhb", 32 * N, ["hbd"], ["row0"], T.row0[p:p + 1, P:IT], T.hbd[96:112, :])

    for n in (256, 512, 1024):
        copy(["yt"], ["yt"], T.yt[:, n:2 * n], T.yt[:, 0:n], "a", n)
    copy(["yt"], ["xt"], T.xt[:, 0:NP], T.yt[:, :], "a")
    wr["xf"] = wr["xt"]
    copy(["yt"], ["v1"], b("v1"), T.yt[:, 0:CH], "a", NP)

    iota("jm", b("jm"), [[1, 16]], 0, 0)
    iota("pi", b("pi"), [[1, 1]], 0, 1, False)
    iota("gli", b("gli"), [[16, 20]], 0, 1, False)
    iota("gli", b("gli", 0, 16), [[16, 20]], OB, 1, False)
    begin("b48", E1, K1)
    for k, rm, rw in ((1, 128, 24), (0, 16, 8)):
        iota("val.c", b("val", 0, rm, 0, 128), [[32, 8], [1, 16]], S0 + OB + 16 * k, 0)
        iota("val.c", b("val", 0, rw, 0, 128), [[2, 8], [16, 16]], Z + k, 0)
        iota("val.v", b("val", 0, rm, 128, 160), [[32, 2], [1, 16]], S0 + VB + 16 * k, 0)
        iota("val.v", b("val", 0, rw, 128, 160), [[8, 2], [1, 4], [16, 4]], Z + P + 4 * k, 0)

    def compact(n, marks, key, base, width, of, val, vkeys, pl):
        k = n // 32

        def s(name, w=k):
            return b(name, 0, 32, 0, w)
        scan(["ones", base, key], ["pf"], s("pf", n), s("ones", n), marks, b(base, 0, 32))
        tt(["pf", key], ["qq"], s("qq", n), s("pf", n), marks, A.mult)
        op("v", g.vector.transpose, ["qq"], ["tq"], s("tq", n), s("qq", n))
        scan(["tq", "k32"], ["ts"], s("ts", n), s("k32", n), s("tq", n), 0.0)
        u = T.ts[0:32, 31:n:32]
        tsc(["ts"], ["hi"], s("hi"), u, 1.0 / 16, A.mult, -0.46875, A.add)
        tsc(["ts"], ["lo"], s("lo"), u, float(width), A.mult)
        tsc(["hi"], ["l2"], s("l2"), s("hi"), 1.0 - 16.0 * width, A.mult)
        tt(["l2", "lo"], ["sm2"], s("sm2"), s("l2"), s("lo"), A.add)
        tt(["sm2", "dd"], ["mx2"], s("mx2"), s("sm2"), s("dd"), A.max)
        copy(["mx2"], [of], s(of), s("mx2"))
        copy([of] + vkeys, [pl], T[pl][:, :].indirect(T[of][:, 0:k]), T[val][:, :])

    def wrap(k):
        c, a = CC[k], KK[k]
        both = [("dpm", 8, ("ma", "mb")), ("dpl", 0, ("la", "lb"))]
        for sem, r, nms in both if k == "1" else both[::-1]:
            for i, nm in enumerate(nms):
                dma("y", sem + k, 32, ["pl" + k], [nm + k], b(nm + k), T["pl" + k][16 * i + r:16 * i + r + 8, a:a + 16 * c])

    for r1, nm, plus in ((32, "vm0", 16), (24, "vp0", 4), (16, "vm0", 0), (8, "vp0", 0)):
        tsc([nm], ["val0"], b("val0", 0, r1), b(nm, 0, r1), float(plus), A.add)
    fill("pl0", b("pl0", 0, 8, K0, K0 + 16 * C0), 0.0)
    tsc(["row1"], ["hb1"], T.hb1[0:N, :], T.row1[0:N, :], 8, A.arith_shift_right)
    tsc(["hb1", "dcol"], ["md1"], T.md1[0:N, :], T.hb1[0:N, :], b("dcol", 0, N), A.is_equal)
    compact(V, T.md1[0:32, :], "md1", "b16", C0, "ofp0", "val0", ["val0"], "pl0")
    wrap("0")
    for p in range(N):
        dma("y", "demp", 16 * N, ["idd", "xf"], ["xo"], T.xt[p:p + 1, OB:OB + P], T.idd[:, :])
    op("v", g.vector.quantize_mx, ["cv.z", "cv.c"], ["qo.own"], T.qo[:, 0:OWN], T.qos[:, 0:OWN], T.cv[:, :])
    copy(["gli"], ["gl"], T.gl[:, 0:16], T.gli[:, 0:16])
    sb("pm", "pi", 15, A.bitwise_and)
    copy(["pm"], ["pmf"], b("pmf"), b("pm"))
    tsc(["jm", "pmf"], ["mask"], T.mask[:, 0:16], b("jm"), b("pmf"), A.is_equal)
    tsc(["row0", "dcol"], ["md"], T.md[0:N, :], T.row0[0:N, :], b("dcol", 0, N), A.is_equal)

    arrive("aL", "lfar")
    for r in range(N):
        dma("y", "df1", 128, ["lfar", "lown"], ["f1f"], T.f1f[0:32, 4 * r:4 * r + 4], T.lists[r, 64:96, :])
    for h in range(2):
        p = 16 * h + AD
        dma("a", "dfan", 32, ["lfar", "lown"], ["xt"], T.xt[p:p + 1, 0:NP], T.lists[:, 0:64, :])
    for h in range(2):
        p = 16 * h + AD
        dma("a", "dv1", 32, ["lfar", "lown"], ["v1"], T.v1[p:p + 1, :], T.lists[:, 96 + 16 * h:112 + 16 * h, :])
    load_w("y", 0)
    load_w("y", 1)
    dma("y", "dfw", 32, ["qo.own"], ["fw.own"], T.fw[:, 0:OWN].bitcast(dt.uint8), T.qo[:, 0:OWN].bitcast(dt.uint8))
    dma("y", "dfw", 32, ["qo.own"], ["fw.own"], T.fws[:, 0:OWN], T.qos[:, 0:OWN])
    copy(["yt"], ["x1"], T.xt[:, NP:2 * NP], T.yt[:, :], "a", 2 * NP)

    def look(table, keys, of, ok, gm, gk, n):
        tt(keys + [ok, "mask"], [gk], gm, table.indirect(of), T.mask[:, 0:n], A.mult)

    X = ["xt", "x1", "x2"]

    def step(t, of, gm):
        copy(X[0:t + 1] + ["xo", of], [gm], b(gm), T.xt[:, 0:NP * (t + 1)].indirect(b(of)))

    def turn(gm, of):
        op("v", g.vector.transpose, [gm], ["tr"], T.tr[0:32, :], T[gm][0:32, :])
        copy(["tr"], [of], b(of, 0, 32), T.tr[0:32, AD:CH:16])

    def put(t, of, val):
        copy([of, val], X[0:t + 1], T.xt[:, 0:NP * (t + 1)].indirect(b(of)), b(val))

    def picks(k):
        la, lb, ma, mb, pku, dst, px, mt = [x + k for x in ("la", "lb", "ma", "mb", "pk", "sn", "px", "mt")]
        pku, dss, mtu = pku + "u", dst + "s", mt + "u"

        def slots_of():
            tb(mt, ma, mb, A.max)
            copy([mt], [mtu], b(mtu), b(mt))
        if k == "1":
            slots_of()
        tb(px, la, lb, A.max)
        copy([px], [pku], b(pku), b(px))
        copy(["qo.own", pku], [dst], b(dst).bitcast(dt.uint32), b("qo").bitcast(dt.uint32).indirect(b(pku)))
        copy(["qo.own", pku], [dss], b(dss), b("qos").indirect(b(pku)), "a")
        if k == "0":
            slots_of()

    def send(k, first, e):
        mtu, meta, dst, dss, w = "mt" + k + "u", "meta" + k, "sn" + k, "sn" + k + "s", W[k]
        need("g", wr[mtu])
        spread("aM" + k, lambda d: (T[mtu][:, w * at(d, me):w * at(d, me) + w], T[meta][:, w * at(me, d):w * at(me, d) + w]))
        need("g", wr[dst])
        spread("aC" + k, lambda d: (T[dst][:, e * at(d, me):e * at(d, me) + e].bitcast(dt.uint8),
                                    T.fw[:, first + e * at(me, d):first + e * at(me, d) + e].bitcast(dt.uint8)))
        need("g", wr[dss])
        spread("aS" + k, lambda d: (T[dss][:, e * at(d, me):e * at(d, me) + e],
                                    T.fws[:, first + e * at(me, d):first + e * at(me, d) + e]))
        arrive("aM" + k, meta)
        arrive("aC" + k, "fw" + k)
        arrive("aS" + k, "fws" + k)

    picks("0")
    copy(["f1f"], ["of1"], b("of1", 0, 32), b("f1f", 0, 32))
    copy(["yt", "of1"], ["v2"], b("v2"), b("yt").indirect(b("of1")), "a")
    step(0, "of1", "gm0")
    need("g", wr["of1"])
    send("0", OWN, E0)
    iota("a0", b("a0", 0, 128, 0, P), [[1, P]], OB, 0)
    iota("a0.v", b("a0", 0, 128, P, IT), [[1, V]], VB, 0)
    iota("pl1", b("pl1", 0, 32, K1, K1 + 16 * C1), [[0, 16 * C1]], 0, 0)
    iota("pl1", b("pl1", 0, 16, K1, K1 + 16 * C1), [[1, 16], [0, N - 1], [16, 3]], E1 * me, 0)
    iota("pl1", b("pl1", 0, 8, K1, K1 + 16 * C1), [[0, 16 * C1]], 0, 0)
    iota("slot.own", b("slot", 0, 128, S0 + OB, S0 + OB + P), [[1, 16], [16, 16]], Z, 0)
    iota("slot.own", b("slot", 0, 128, S0 + VB, S0 + VB + V), [[1, 16], [16, 4]], Z + P, 0)
    iota("sl0", b("sl0"), [[1, (N - 1) * E0]], OWN, 0)
    iota("sl1", b("sl1"), [[1, (N - 1) * E1]], W1, 0)

    OX = T.xt[0:16, OB:OB + P]
    put(0, "of1", "v1")
    copy(["xt"], ["x1s"], T.x1s[0:16, :], OX, "a")
    copy(["yt"], ["x2"], T.xt[:, 2 * NP:3 * NP], T.yt[:, :], "a", 2 * NP)
    turn("gm0", "ofq")
    step(1, "ofq", "gm1")
    put(1, "ofq", "v2")
    copy(["xt"], ["x2s"], T.x2s[0:16, :], OX, "a")
    turn("gm1", "ofz")
    step(2, "ofz", "gm2")
    copy(["of1"], ["gl.v"], T.gl[:, 16:20], T.of1[:, 4 * me:4 * me + 4])
    put(2, "ofz", "gm1")

    tt(["xt", "gl", "gl.v", "a0", "a0.v"], ["ei"], b("ei"), T.xt[:, 0:NP].indirect(b("gl")), b("a0"), A.not_equal)
    tt(["ei", "md"], ["gg"], T.gg[0:32, :], T.ei[0:32, :], T.md[0:32, :], A.mult)
    compact(IT, T.gg[0:32, :], "gg", "b48", C1, "ofp", "val", ["val.c", "val.v"], "pl1")
    for t, nm in enumerate(("x1s", "x2s")):
        dma("y", "di%d" % t, 16, [nm], ["idw%d" % t], T.idw[:, 16 * t:16 * t + 16], T[nm][0:8, :])
    wrap("1")
    copy(["xt"], ["x3s"], T.x3s[0:16, :], OX, "a")
    dma("y", "di2", 16, ["x3s"], ["idw2"], T.idw[:, 32:48], T.x3s[0:8, :])
    for nm in ("mask", "keep"):
        n = 16
        while n < CH:
            copy([nm], [nm], T[nm][:, n:2 * n], T[nm][:, 0:n], "a")
            n *= 2

    def fill_slots(k):
        copy(["meta" + k, "sl" + k], ["slot", "slot.own", "slot.z"],
             b("slot").indirect(T["meta" + k][:, 0:W[k] * (N - 1)]), b("sl" + k))

    def slots(keys, c0, c1):
        tsc(keys, ["idu%d" % t for t in range(c0, c1, 16)], T.idu[:, c0:c1], T.idw[:, c0:c1], float(S0), A.add)

    def stand(c0, c1):
        gk, w, n = "gs%d" % c0, slice(16 * c0, 16 * c1), 16 * (c1 - c0)
        look(b("slot"), ["slot", "slot.own", "slot.z"], T.idu[:, c0:c1], "idu%d" % c0, T.gs[:, w], gk, n)
        scan([gk, "keep"], [gk + "c"], T.gsc[:, w], T.keep[:, 0:n], T.gs[:, w], 0.0)
        op("v", g.vector.tensor_copy, [gk + "c"], ["so%d" % t for t in range(c0 // 16, c1 // 16)], T.so[:, c0:c1],
           T.gsc[:, 16 * c0 + 15:16 * c1:16])

    def place(t):
        copy(["fw.own", "so%d" % t] + ["fw%d" % k for k in range(min(t, 1) + 1)], ["pk%d" % t], b("pk%d" % t).bitcast(dt.uint32),
             T.fw[:, 0:WW if t else W1].bitcast(dt.uint32).indirect(T.so[:, 16 * t:16 * t + 16]))

    def products(t):
        pk, ps = "pk%d" % t, "ps%d" % t
        copy(["fw.own", "so%d" % t] + ["fws%d" % k for k in range(min(t, 1) + 1)], [ps], b(ps),
             T.fws[:, 0:WW if t else W1].indirect(T.so[:, 16 * t:16 * t + 16]), "a")
        for i in range(O * t, O * t + O):
            w = slice(128 * i, 128 * i + 128)
            op("p", g.tensor.matmul_mx, ["wq%d" % (i // 4), pk, ps], ["acc%d" % i], T.acc[:, 512 * i:512 * i + P],
               T.wq[:, w], T.wqs[:, w], b(pk), b(ps), True, True)

    def out(t, es):
        for o in range(O):
            i = O * t + o
            w = slice(P * i, P * i + P)
            copy(["acc%d" % i], ["ys%d" % i], T.ys[:, w], T.acc[:, 512 * i:512 * i + P], es[o])
            dma("y", "dy", 16 * R * O, ["ys%d" % i], ["y%d" % i], T.y[:, w], T.ys[:, w])

    turn("gm2", "ofw")
    put(2, "ofw", "gm2")
    picks("1")
    send("1", W1, E1)
    dma("y", "di3", 16, ["xt"], ["idw3"], T.idw[:, 48:64], T.xt[0:8, OB:OB + P])
    slots(["idw0", "idw1", "idw2"], 0, 48)
    fill_slots("0")
    stand(0, 16)
    place(0)
    pack(0)
    products(0)
    out(0, "aa")
    fill_slots("1")
    slots(["idw3"], 48, 64)
    stand(16, 48)
    place(1)
    products(1)
    place(2)
    pack(1)
    products(2)
    out(1, "aa")
    stand(48, 64)
    place(3)
    products(3)
    out(2, "va")
    out(3, "va")
    need("y", [("dy", 16 * R * O)])
    need("g", [("lsent", sent[0])])
